import numpy as np
import ml_dtypes


def mxq(x, axis, fmt="e4m3"):
    dtype, down = {"e4m3": (ml_dtypes.float8_e4m3fn, 7), "e5m2": (ml_dtypes.float8_e5m2, 14)}[fmt]
    v = np.moveaxis(np.asarray(x, np.float32).astype(ml_dtypes.bfloat16).astype(np.float64), axis, -1)
    blocks = v.reshape(v.shape[:-1] + (-1, 32))
    amax = np.abs(blocks).max(-1, keepdims=True)
    byte = np.maximum(np.where(amax > 0, np.frexp(amax)[1] - 1 + 127, 0) - down, 1)
    scale = np.exp2(byte - 127.0)
    codes = (blocks / scale).astype(np.float32).astype(dtype).astype(np.float64)
    return np.moveaxis((codes * scale).reshape(v.shape), -1, axis)


WIDE = False


def mx_kscale(k):
    if not WIDE:
        return np.ones(k)
    levels = np.array([10, -10, 5, -5, 0])
    if k % 512:
        return np.exp2(np.random.permutation(np.resize(levels, k // 32))).repeat(32)
    a = np.empty((k // 512, 16))
    for p in range(k // 512):
        a[p, :8] = np.random.permutation(np.resize(levels, 8))
        for g in range(8):
            far = levels[np.abs(levels - a[p, g]) >= 10]
            a[p, g + 8] = far[np.random.randint(len(far))]
    return np.exp2(a.ravel()).repeat(32)


def f64(x):
    return np.asarray(x).astype(np.float64)


def striped(idx):
    return np.tile(idx.reshape(-1, 16).T, (8, 1)).astype(np.uint16)


def unstriped(offs):
    return offs[:16].T.reshape(-1).astype(np.int64)


E2M1 = np.array([0.0, 0.5, 1.0, 1.5, 2.0, 3.0, 4.0, 6.0, -0.0, -0.5, -1.0, -1.5, -2.0, -3.0, -4.0, -6.0])


def pack_weight(w, fmt):
    k, n = w.shape
    w = f64(np.asarray(w, np.float32).astype(ml_dtypes.bfloat16)).reshape(k // 32, 32, n)
    amax = np.abs(w).max(1)
    if fmt == "e4m3":
        byte = np.frexp(amax)[1] - 1 + 127 - 7
    else:
        mant, ex = np.frexp(amax / 6.0)
        byte = np.where(mant > 0.5, ex, ex - 1) + 127
    byte = np.clip(np.where(amax > 0, byte, 1), 1, 254)
    scaled = (w * np.exp2(127.0 - byte)[:, None, :]).reshape(k, n).astype(np.float32)
    by_word = np.ascontiguousarray(scaled.reshape(k // 512, 128, 4, n).transpose(0, 1, 3, 2))
    if fmt == "e4m3":
        words = by_word.astype(ml_dtypes.float8_e4m3fn).view(np.uint8)
    else:
        c = by_word.astype(ml_dtypes.float4_e2m1fn).view(np.uint8) & 0xF
        words = (c[..., 0::2] | (c[..., 1::2] << 4)).reshape(k // 512, 128, 2 * n)
    return np.ascontiguousarray(words), np.ascontiguousarray(byte.astype(np.uint8).reshape(k // 512, 16, n))


def unpack_weight(words, scales, fmt):
    g, _, n = scales.shape
    words = np.ascontiguousarray(words).reshape(g, 128, n, -1)
    if fmt == "e4m3":
        vals = words.view(ml_dtypes.float8_e4m3fn).astype(np.float64)
    else:
        nib = np.empty((g, 128, n, 4), np.uint8)
        nib[..., 0::2] = words & 0xF
        nib[..., 1::2] = words >> 4
        vals = E2M1[nib]
    vals = vals * np.repeat(np.exp2(scales.astype(np.float64) - 127.0), 8, axis=1)[..., None]
    return vals.transpose(0, 1, 3, 2).reshape(g * 512, n)


def relu2(v):
    return np.maximum(v, 0.0) ** 2


K, T, E, C, H, N = 1024, 640, 4, 128, 512, 384


def by_expert(wq, xq):
    return np.concatenate([wq[e].T @ xq[:, e * C:(e + 1) * C] for e in range(E)], axis=1)


def setup_inputs():
    n = np.random.standard_normal
    s = mx_kscale(K)[:, None]
    u = mx_kscale(H)
    x = pack_weight(n((K, T)) * s, "e4m3")
    return {
        "x_words": x[0],
        "x_scales": x[1],
        "w1": (n((E, K, H)) / np.sqrt(K) / s[None] * u[None, None, :]).astype(np.float32),
        "w2": (n((E, H, N)) / np.sqrt(H) / u[None, :, None] ** 2).astype(np.float32),
        "gate": np.tile(np.random.uniform(0.2, 1.0, E * C), (N, 1)).astype(np.float32),
        "offs": striped(np.random.permutation(T)[:E * C]),
        "dst": striped(np.random.permutation(T)[:E * C]),
    }


def reference(x_words, x_scales, w1, w2, gate, offs, dst):
    idx = unstriped(offs)
    xq = unpack_weight(x_words, x_scales, "e4m3")[:, idx]
    h = relu2(by_expert(mxq(f64(w1), 1, "e4m3"), xq))
    y = by_expert(mxq(f64(w2), 1, "e4m3"), mxq(h, 0, "e4m3"))
    out = np.zeros((N, T))
    out[:, unstriped(dst)] = f64(gate) * y
    return out

@@ -1,0 +1,218 @@
+from contextlib import ExitStack
+
+import concourse.mybir as mybir
+
+K, T, E, C, H, N = 1024, 640, 4, 128, 512, 384
+
+F32 = mybir.dt.float32
+BF16 = mybir.dt.bfloat16
+I32 = mybir.dt.int32
+U32 = mybir.dt.uint32
+U16 = mybir.dt.uint16
+U8 = mybir.dt.uint8
+FP8X4 = mybir.dt.float8_e4m3fn_x4
+ACT = mybir.ActivationFunctionType
+MULT = mybir.AluOpType.mult
+
+P = 128
+PACK = 4
+PASSES = K // (P * PACK)
+SLOTS = E * C
+CHUNKS = N // P
+LIST_COLS = C // 16
+HALF = SLOTS // 2
+W1_SCALAR = (56, 32, 72, 48, 112, 104, 32, 120)
+W2_SCALAR = (224, 128, 128, 128)
+FUSED = (False, False, False, False)
+SPLIT = 1
+SQUARE_V = (False, False, False, False)
+LOADS = "a00 d a01 s a11 b00 a10 g0 b10 a20 a21 a31 a30 b20 b30 b31 b32 g1"
+STEPS = "G1 R30 r21 R00 r00 r20 r01 r10 q00 q10 R10 r11 G0 q11 r30 q01 R31 q21 f1 f0 h0 h1 Q00 Q10 Q31 m10 q30 R32 m00 R20 q20 r31 q31 Q20 f2 h2 f3 p00 h3 Q32 p10 m32 x00 m20 x10 p20 Q30 m31 x20 p32 x32 p31 m30 p30 x30 x31 o1 o2 o0"
+
+FLOPS = 2 * SLOTS * (K * H + H * N)
+
+
+def tile_moe_two_mlp_relu2_kernel(tc, x_words, x_scales, w1, w2, gate, offs, dst, out):
+    nc = tc.nc
+    last = E - 1
+
+    with ExitStack() as ctx:
+        keep = ctx.enter_context(tc.tile_pool(name="keep", bufs=1))
+        psum = ctx.enter_context(tc.psum_pool(name="psum", bufs=1))
+
+        def sbuf(name, shape, dtype):
+            return keep.tile(shape, dtype, name=name, align_bytes=64)
+
+        offs_sb = keep.tile([P, SLOTS // 16], U16, name="offs_sb")
+        dst_sb = keep.tile([P, SLOTS // 16], U16, name="dst_sb")
+        tok_words = sbuf("tok_words", [P, PASSES * T], I32)
+        tok_scales = sbuf("tok_scales", [P, T], U8)
+        slot_words = sbuf("slot_words", [P, PASSES, SLOTS], U32)
+        slot_scales = sbuf("slot_scales", [P, SLOTS], U8)
+        gate_sb = [sbuf(f"gate{u}", [P, CHUNKS, HALF], F32) for u in range(2)]
+        out_sb = [sbuf(f"out{c}", [P, T], F32) for c in range(CHUNKS)]
+
+        w1_raw = [[sbuf(f"w1raw{e}_{o}", [P, PACK, H], F32) for o in range(PASSES)] for e in range(E)]
+        w1_bf = [[sbuf(f"w1bf{e}_{o}", [P, PACK, P, PACK], BF16) for o in range(PASSES)] for e in range(E)]
+        w1_words = [[sbuf(f"w1w{e}_{o}", [P, H], U32) for o in range(PASSES)] for e in range(E)]
+        w1_scales = [[sbuf(f"w1s{e}_{o}", [P, H], U8) for o in range(PASSES)] for e in range(E)]
+        pieces = [[(0, N)] for e in range(last)] + [[(c * P, P) for c in range(CHUNKS)]]
+        w2_raw = [[sbuf(f"w2raw{e}_{n0}", [P, PACK, w], F32) for n0, w in pieces[e]] for e in range(E)]
+        w2_bf = [[sbuf(f"w2bf{e}_{n0}", [P, w, PACK], BF16) for n0, w in pieces[e]] for e in range(E)]
+        w2_words = [[sbuf(f"w2w{e}_{n0}", [P, w], U32) for n0, w in pieces[e]] for e in range(E)]
+        w2_scales = [[sbuf(f"w2s{e}_{n0}", [P, w], U8) for n0, w in pieces[e]] for e in range(E)]
+        relu_sb = [sbuf(f"relu{e}", [P, C, PACK], F32) for e in range(E)]
+        h_bf = [sbuf(f"hbf{e}", [P, C * PACK], BF16) for e in range(E)]
+        h_words = [sbuf(f"hw{e}", [P, C], U32) for e in range(E)]
+        h_scales = [sbuf(f"hs{e}", [P, C], U8) for e in range(E)]
+        gated = [[sbuf(f"gated{e}_{n0}", [P, w // P, C], F32) for n0, w in pieces[e]] for e in range(E)]
+        a_ps = [psum.tile([P, PACK, C], F32, name=f"a{e}", tag=f"a{e % 2}") for e in range(E)]
+        y_ps = [[psum.tile([P, w // P, C], F32, name=f"y{e}_{n0}") for n0, w in pieces[e]] for e in range(E)]
+
+        def load_w1(e, o):
+            rows = w1[e, o * P * PACK : (o + 1) * P * PACK, :]
+            nc.sync.dma_start(out=w1_raw[e][o][:], in_=rows.rearrange("(p j) i -> p j i", j=PACK))
+
+        def load_w2(e, q):
+            n0, w = pieces[e][q]
+            nc.sync.dma_start(out=w2_raw[e][q][:], in_=w2[e, :, n0 : n0 + w].rearrange("(p j) n -> p j n", j=PACK))
+
+        def load_gate(u):
+            cols = gate[:, u * HALF : (u + 1) * HALF]
+            nc.sync.dma_start(out=gate_sb[u][:], in_=cols.rearrange("(c p) s -> p c s", p=P))
+
+        nc.vector.memset(tok_scales[:].bitcast(I32), 0)
+        for c in range(CHUNKS):
+            nc.gpsimd.memset(out_sb[c][:], 0.0)
+
+        def load_scales():
+            for q in range(4):
+                nc.sync.dma_start(
+                    out=tok_scales[32 * q : 32 * q + 4 * PASSES, :].bitcast(I32),
+                    in_=x_scales[:, 4 * q : 4 * q + 4, :].bitcast(I32),
+                )
+
+        nc.sync.dma_start(
+            out=tok_words[:].rearrange("p (o t) -> p o t", o=PASSES),
+            in_=x_words.rearrange("o p t r -> p o (t r)").bitcast(I32),
+        )
+        nc.sync.dma_start(offs_sb[:], offs)
+        loaders = {"a": load_w1, "b": load_w2, "g": load_gate, "s": load_scales, "d": lambda: nc.sync.dma_start(dst_sb[:], dst)}
+        for item in LOADS.split():
+            loaders[item[0]](*[int(ch) for ch in item[1:]])
+
+        def gather(u):
+            cols = slice(u * HALF, (u + 1) * HALF)
+            lst = offs_sb[:, u * HALF // 16 : (u + 1) * HALF // 16]
+            for o in range(PASSES):
+                window = tok_words[:, o * T : (o + 1) * T].bitcast(U32)
+                nc.vector.tensor_copy(slot_words[:, o, cols], window.indirect(lst))
+            nc.vector.tensor_copy(slot_scales[:, cols], tok_scales[:].indirect(lst))
+
+        def round_w1(e, o):
+            src = w1_raw[e][o][:].rearrange("p j (m t) -> p m j t", t=PACK)
+            dest = w1_bf[e][o][:].rearrange("p t m j -> p m j t")
+            cut = W1_SCALAR[e * PASSES + o]
+            edges = [4 * (cut // 4 * s // SPLIT) for s in range(SPLIT + 1)]
+            for a, b in zip(edges, edges[1:]):
+                if b > a:
+                    nc.scalar.activation(out=dest[:, a:b], in_=src[:, a:b], func=ACT.Copy)
+            if cut < P:
+                nc.vector.tensor_copy(out=dest[:, cut:], in_=src[:, cut:])
+
+        def quant_w1(e, o):
+            nc.vector.quantize_mx(
+                out=w1_words[e][o][:].bitcast(FP8X4),
+                scales=w1_scales[e][o][:],
+                in_=w1_bf[e][o][:].rearrange("p t m j -> p (t m j)"),
+            )
+
+        def first_layer(e):
+            slots = slice(e * C, (e + 1) * C)
+            for t in range(PACK):
+                cols = slice(t * P, (t + 1) * P)
+                for o in range(PASSES):
+                    nc.tensor.matmul_mx(
+                        out=a_ps[e][:, t, :],
+                        lhsT=w1_words[e][o][:, cols].bitcast(FP8X4),
+                        lhsT_scale=w1_scales[e][o][:, cols],
+                        rhs=slot_words[:, o, slots].bitcast(FP8X4),
+                        rhs_scale=slot_scales[4 * o :, slots],
+                        start=(o == 0),
+                        stop=(o == PASSES - 1),
+                    )
+            nc.scalar.activation(out=relu_sb[e][:], in_=a_ps[e][:].rearrange("p t s -> p s t"), func=ACT.Relu)
+            flat = relu_sb[e][:].rearrange("p s t -> p (s t)")
+            if SQUARE_V[e]:
+                nc.vector.tensor_tensor(out=h_bf[e][:], in0=flat, in1=flat, op=MULT)
+            else:
+                nc.scalar.activation(out=h_bf[e][:], in_=flat, func=ACT.Square)
+
+        def quant_h(e):
+            nc.vector.quantize_mx(out=h_words[e][:].bitcast(FP8X4), scales=h_scales[e][:], in_=h_bf[e][:])
+
+        def round_w2(e, q):
+            scalar_cols = W2_SCALAR[e]
+            src = w2_raw[e][q][:].rearrange("p j (b i) -> p b j i", i=4)
+            dest = w2_bf[e][q][:].rearrange("p (b i) j -> p b j i", i=4)
+            cut = scalar_cols // 4
+            if cut > 0:
+                nc.scalar.activation(out=dest[:, :cut], in_=src[:, :cut], func=ACT.Copy)
+            if scalar_cols < pieces[e][q][1]:
+                nc.vector.tensor_copy(out=dest[:, cut:], in_=src[:, cut:])
+
+        def quant_w2(e, q):
+            w = pieces[e][q][1]
+            for a, b in ((0, min(w, 256)), (256, w)):
+                if b > a:
+                    nc.vector.quantize_mx(
+                        out=w2_words[e][q][:, a:b].bitcast(FP8X4),
+                        scales=w2_scales[e][q][:, a:b],
+                        in_=w2_bf[e][q][:, a:b, :].rearrange("p n j -> p (n j)"),
+                    )
+
+        def second_layer(e, q):
+            n0, w = pieces[e][q]
+            for c in range(w // P):
+                cols = slice(c * P, (c + 1) * P)
+                nc.tensor.matmul_mx(
+                    out=y_ps[e][q][:, c, :],
+                    lhsT=w2_words[e][q][:, cols].bitcast(FP8X4),
+                    lhsT_scale=w2_scales[e][q][:, cols],
+                    rhs=h_words[e][:].bitcast(FP8X4),
+                    rhs_scale=h_scales[e][:],
+                    start=True,
+                    stop=True,
+                )
+
+        def apply_gate(e, q):
+            n0, w = pieces[e][q]
+            c0 = n0 // P
+            s0 = (e * C) % HALF
+            if FUSED[e]:
+                nc.scalar.activation(out=gated[e][q][:], in_=y_ps[e][q][:], func=ACT.Copy)
+                return
+            nc.vector.tensor_tensor(
+                out=gated[e][q][:],
+                in0=y_ps[e][q][:],
+                in1=gate_sb[e * C // HALF][:, c0 : c0 + w // P, s0 : s0 + C],
+                op=MULT,
+            )
+
+        def scatter(e, q):
+            n0, w = pieces[e][q]
+            lst = dst_sb[:, e * LIST_COLS : (e + 1) * LIST_COLS]
+            for c in range(w // P):
+                window = out_sb[n0 // P + c][:].indirect(lst)
+                if FUSED[e]:
+                    s0 = (e * C) % HALF
+                    nc.vector.tensor_tensor(window, gated[e][q][:, c, :], gate_sb[e * C // HALF][:, n0 // P + c, s0 : s0 + C], MULT)
+                else:
+                    nc.vector.tensor_copy(window, gated[e][q][:, c, :])
+
+        def store(c):
+            nc.sync.dma_start(out=out[c * P : (c + 1) * P, :], in_=out_sb[c][:])
+
+        stages = {"G": gather, "r": round_w1, "q": quant_w1, "f": first_layer, "h": quant_h, "R": round_w2, "Q": quant_w2, "m": second_layer, "p": apply_gate, "x": scatter, "o": store}
+        for item in STEPS.split():
+            stages[item[0]](*[int(ch) for ch in item[1:]])

@@ -21,13 +21,20 @@ SLOTS = E * C
 CHUNKS = N // P
 LIST_COLS = C // 16
 HALF = SLOTS // 2
-W1_SCALAR = (56, 32, 72, 48, 112, 104, 32, 120)
-W2_SCALAR = (224, 128, 128, 128)
-FUSED = (False, False, False, False)
-SPLIT = 1
+W1_SCALAR = (80, 80, 64, 80, 56, 128, 16, 80)
+W2_SCALAR = (256, 288, 32, 32)
+FUSED = (True, True, True, True)
+TAGS = {}
+SCQ = False
+QSPLIT = (True, False, False, False)
+YSPLIT = (True, True, False, False)
+RV = (1, 2, 0, 0)
+W2_POOL = (0, 0, 0, 0)
+GN = 2
+GATE4 = False
 SQUARE_V = (False, False, False, False)
-LOADS = "a00 d a01 s a11 b00 a10 g0 b10 a20 a21 a31 a30 b20 b30 b31 b32 g1"
-STEPS = "G1 R30 r21 R00 r00 r20 r01 r10 q00 q10 R10 r11 G0 q11 r30 q01 R31 q21 f1 f0 h0 h1 Q00 Q10 Q31 m10 q30 R32 m00 R20 q20 r31 q31 Q20 f2 h2 f3 p00 h3 Q32 p10 m32 x00 m20 x10 p20 Q30 m31 x20 p32 x32 p31 m30 p30 x30 x31 o1 o2 o0"
+LOADS = "x f a00 s a01 b0 a10 g0 g1 d g3 b1 a11 a30 a20 a21 a31 b2 b3 g2"
+STEPS = "r210 G3 r100 r111 G1 r201 r110 R10 r000 q11 r200 r010 R01 r011 R02 r310 r301 R12 r001 r300 q00 r101 R11 q01 G0 R00 f0 q10 r211 q21 R32 R20 R31 u0 r311 f1 u1 q30 q31 v0 R21 h0 v1 G2 q20 R22 Q0 m0 Q1 f2 u2 h1 v2 p0 m1 h2 f3 x00 x02 u3 v3 Q2 p1 x12 h3 R30 Q3 m2 p2 x01 x10 m3 p3 x11 x20 x31 x30 x22 o0 x32 x21 o2 o1"
 
 FLOPS = 2 * SLOTS * (K * H + H * N)
 
@@ -43,43 +50,62 @@ def tile_moe_two_mlp_relu2_kernel(tc, x_words, x_scales, w1, w2, gate, offs, dst
         def sbuf(name, shape, dtype):
             return keep.tile(shape, dtype, name=name, align_bytes=64)
 
+        made = {}
+
+        def buf(name, shape, dtype):
+            if name not in made:
+                made[name] = keep.tile(shape, dtype, name=name, tag=TAGS.get(name, name), align_bytes=64)
+            return made[name]
+
         offs_sb = keep.tile([P, SLOTS // 16], U16, name="offs_sb")
         dst_sb = keep.tile([P, SLOTS // 16], U16, name="dst_sb")
         tok_words = sbuf("tok_words", [P, PASSES * T], I32)
         tok_scales = sbuf("tok_scales", [P, T], U8)
         slot_words = sbuf("slot_words", [P, PASSES, SLOTS], U32)
         slot_scales = sbuf("slot_scales", [P, SLOTS], U8)
-        gate_sb = [sbuf(f"gate{u}", [P, CHUNKS, HALF], F32) for u in range(2)]
+        gate_sb = lambda u: buf(f"gate{u}", [P, CHUNKS, C if GATE4 else HALF], F32)
         out_sb = [sbuf(f"out{c}", [P, T], F32) for c in range(CHUNKS)]
 
-        w1_raw = [[sbuf(f"w1raw{e}_{o}", [P, PACK, H], F32) for o in range(PASSES)] for e in range(E)]
-        w1_bf = [[sbuf(f"w1bf{e}_{o}", [P, PACK, P, PACK], BF16) for o in range(PASSES)] for e in range(E)]
+        w1_raw = lambda e, o: buf(f"w1raw{e}{o}", [P, PACK, H], F32)
+        w1_bf = lambda e, o: buf(f"w1bf{e}{o}", [P, PACK, P, PACK], BF16)
         w1_words = [[sbuf(f"w1w{e}_{o}", [P, H], U32) for o in range(PASSES)] for e in range(E)]
         w1_scales = [[sbuf(f"w1s{e}_{o}", [P, H], U8) for o in range(PASSES)] for e in range(E)]
-        pieces = [[(0, N)] for e in range(last)] + [[(c * P, P) for c in range(CHUNKS)]]
-        w2_raw = [[sbuf(f"w2raw{e}_{n0}", [P, PACK, w], F32) for n0, w in pieces[e]] for e in range(E)]
-        w2_bf = [[sbuf(f"w2bf{e}_{n0}", [P, w, PACK], BF16) for n0, w in pieces[e]] for e in range(E)]
+        pieces = [[(0, N)] for e in range(E)]
+        w2_raw = lambda e, q: buf(f"w2raw{e}{q}", [P, PACK, pieces[e][q][1]], F32)
+        w2_bf = lambda e, q: buf(f"w2bf{e}{q}", [P, pieces[e][q][1], PACK], BF16)
         w2_words = [[sbuf(f"w2w{e}_{n0}", [P, w], U32) for n0, w in pieces[e]] for e in range(E)]
         w2_scales = [[sbuf(f"w2s{e}_{n0}", [P, w], U8) for n0, w in pieces[e]] for e in range(E)]
-        relu_sb = [sbuf(f"relu{e}", [P, C, PACK], F32) for e in range(E)]
-        h_bf = [sbuf(f"hbf{e}", [P, C * PACK], BF16) for e in range(E)]
+        relu_sb = lambda e: buf(f"relu{e}", [P, PACK, C], F32)
+        h_bf = lambda e: buf(f"hbf{e}", [P, C * PACK], BF16)
         h_words = [sbuf(f"hw{e}", [P, C], U32) for e in range(E)]
         h_scales = [sbuf(f"hs{e}", [P, C], U8) for e in range(E)]
-        gated = [[sbuf(f"gated{e}_{n0}", [P, w // P, C], F32) for n0, w in pieces[e]] for e in range(E)]
-        a_ps = [psum.tile([P, PACK, C], F32, name=f"a{e}", tag=f"a{e % 2}") for e in range(E)]
-        y_ps = [[psum.tile([P, w // P, C], F32, name=f"y{e}_{n0}") for n0, w in pieces[e]] for e in range(E)]
+        gated = lambda e, q: buf(f"gated{e}{q}", [P, pieces[e][q][1] // P, C], F32)
+        def bank(name, tag, shape):
+            if name not in made:
+                made[name] = psum.tile(shape, F32, name=name, tag=tag)
+            return made[name]
+
+        a_ps = lambda e, t: bank(f"a{e}{t}", f"a{t}", [P, C])
+
+        def y_ps(e, q, c):
+            n0, w = pieces[e][q]
+            if YSPLIT[e] or w == P:
+                return bank(f"y{e}{q}{c}", f"y{n0 // P + c}", [P, C])[:]
+            return bank(f"y{e}{q}", f"y{3 - e % 2}", [P, w // P, C])[:, c, :]
 
         def load_w1(e, o):
             rows = w1[e, o * P * PACK : (o + 1) * P * PACK, :]
-            nc.sync.dma_start(out=w1_raw[e][o][:], in_=rows.rearrange("(p j) i -> p j i", j=PACK))
+            nc.sync.dma_start(out=w1_raw(e, o)[:], in_=rows.rearrange("(p j) i -> p j i", j=PACK))
 
-        def load_w2(e, q):
+        def load_w2(e, q=0):
             n0, w = pieces[e][q]
-            nc.sync.dma_start(out=w2_raw[e][q][:], in_=w2[e, :, n0 : n0 + w].rearrange("(p j) n -> p j n", j=PACK))
+            nc.sync.dma_start(out=w2_raw(e, q)[:], in_=w2[e, :, n0 : n0 + w].rearrange("(p j) n -> p j n", j=PACK))
 
         def load_gate(u):
-            cols = gate[:, u * HALF : (u + 1) * HALF]
-            nc.sync.dma_start(out=gate_sb[u][:], in_=cols.rearrange("(c p) s -> p c s", p=P))
+            if not GATE4 and u % 2:
+                return
+            cols = gate[:, u * C : u * C + (C if GATE4 else HALF)]
+            nc.sync.dma_start(out=gate_sb(u)[:], in_=cols.rearrange("(c p) s -> p c s", p=P))
 
         nc.vector.memset(tok_scales[:].bitcast(I32), 0)
         for c in range(CHUNKS):
@@ -87,53 +113,59 @@ def tile_moe_two_mlp_relu2_kernel(tc, x_words, x_scales, w1, w2, gate, offs, dst
 
         def load_scales():
             for q in range(4):
-                nc.sync.dma_start(
+                (nc.scalar if SCQ else nc.sync).dma_start(
                     out=tok_scales[32 * q : 32 * q + 4 * PASSES, :].bitcast(I32),
                     in_=x_scales[:, 4 * q : 4 * q + 4, :].bitcast(I32),
                 )
 
-        nc.sync.dma_start(
-            out=tok_words[:].rearrange("p (o t) -> p o t", o=PASSES),
-            in_=x_words.rearrange("o p t r -> p o (t r)").bitcast(I32),
-        )
-        nc.sync.dma_start(offs_sb[:], offs)
-        loaders = {"a": load_w1, "b": load_w2, "g": load_gate, "s": load_scales, "d": lambda: nc.sync.dma_start(dst_sb[:], dst)}
+        def load_x():
+            nc.sync.dma_start(
+                out=tok_words[:].rearrange("p (o t) -> p o t", o=PASSES),
+                in_=x_words.rearrange("o p t r -> p o (t r)").bitcast(I32),
+            )
+
+        loaders = {"a": load_w1, "b": load_w2, "g": load_gate, "s": load_scales, "x": load_x, "f": lambda: nc.sync.dma_start(offs_sb[:], offs), "d": lambda: nc.sync.dma_start(dst_sb[:], dst)}
         for item in LOADS.split():
             loaders[item[0]](*[int(ch) for ch in item[1:]])
 
         def gather(u):
-            cols = slice(u * HALF, (u + 1) * HALF)
-            lst = offs_sb[:, u * HALF // 16 : (u + 1) * HALF // 16]
+            if GN == 2 and u % 2:
+                return
+            width = SLOTS // GN
+            cols = slice(u * C, u * C + width)
+            lst = offs_sb[:, u * C // 16 : (u * C + width) // 16]
             for o in range(PASSES):
                 window = tok_words[:, o * T : (o + 1) * T].bitcast(U32)
                 nc.vector.tensor_copy(slot_words[:, o, cols], window.indirect(lst))
             nc.vector.tensor_copy(slot_scales[:, cols], tok_scales[:].indirect(lst))
 
-        def round_w1(e, o):
-            src = w1_raw[e][o][:].rearrange("p j (m t) -> p m j t", t=PACK)
-            dest = w1_bf[e][o][:].rearrange("p t m j -> p m j t")
+        def round_w1(e, o, on_scalar):
+            src = w1_raw(e, o)[:].rearrange("p j (m t) -> p m j t", t=PACK)
             cut = W1_SCALAR[e * PASSES + o]
-            edges = [4 * (cut // 4 * s // SPLIT) for s in range(SPLIT + 1)]
-            for a, b in zip(edges, edges[1:]):
-                if b > a:
-                    nc.scalar.activation(out=dest[:, a:b], in_=src[:, a:b], func=ACT.Copy)
-            if cut < P:
+            if on_scalar and cut > 0:
+                dest = w1_bf(e, o)[:].rearrange("p t m j -> p m j t")
+                nc.scalar.activation(out=dest[:, :cut], in_=src[:, :cut], func=ACT.Copy)
+            if not on_scalar and cut < P:
+                dest = w1_bf(e, o)[:].rearrange("p t m j -> p m j t")
                 nc.vector.tensor_copy(out=dest[:, cut:], in_=src[:, cut:])
 
         def quant_w1(e, o):
-            nc.vector.quantize_mx(
-                out=w1_words[e][o][:].bitcast(FP8X4),
-                scales=w1_scales[e][o][:],
-                in_=w1_bf[e][o][:].rearrange("p t m j -> p (t m j)"),
-            )
+            step = P if (QSPLIT[e] and o == PASSES - 1) else H
+            flat = w1_bf(e, o)[:].rearrange("p t m j -> p (t m j)")
+            for a in range(0, H, step):
+                nc.vector.quantize_mx(
+                    out=w1_words[e][o][:, a : a + step].bitcast(FP8X4),
+                    scales=w1_scales[e][o][:, a : a + step],
+                    in_=flat[:, a * PACK : (a + step) * PACK],
+                )
 
         def first_layer(e):
             slots = slice(e * C, (e + 1) * C)
-            for t in range(PACK):
-                cols = slice(t * P, (t + 1) * P)
-                for o in range(PASSES):
+            for o in range(PASSES):
+                for t in range(PACK):
+                    cols = slice(t * P, (t + 1) * P)
                     nc.tensor.matmul_mx(
-                        out=a_ps[e][:, t, :],
+                        out=a_ps(e, t)[:],
                         lhsT=w1_words[e][o][:, cols].bitcast(FP8X4),
                         lhsT_scale=w1_scales[e][o][:, cols],
                         rhs=slot_words[:, o, slots].bitcast(FP8X4),
@@ -141,42 +173,61 @@ def tile_moe_two_mlp_relu2_kernel(tc, x_words, x_scales, w1, w2, gate, offs, dst
                         start=(o == 0),
                         stop=(o == PASSES - 1),
                     )
-            nc.scalar.activation(out=relu_sb[e][:], in_=a_ps[e][:].rearrange("p t s -> p s t"), func=ACT.Relu)
-            flat = relu_sb[e][:].rearrange("p s t -> p (s t)")
+
+        def relu(e):
+            for t in range(PACK):
+                if t >= PACK - RV[e]:
+                    nc.vector.tensor_scalar(out=relu_sb(e)[:, t, :], in0=a_ps(e, t)[:], scalar1=0.0, scalar2=None, op0=mybir.AluOpType.max)
+                else:
+                    nc.scalar.activation(out=relu_sb(e)[:, t, :], in_=a_ps(e, t)[:], func=ACT.Relu)
+
+        def square(e):
+            flat = relu_sb(e)[:].rearrange("p t s -> p s t")
+            dest = h_bf(e)[:].rearrange("p (s t) -> p s t", t=PACK)
             if SQUARE_V[e]:
-                nc.vector.tensor_tensor(out=h_bf[e][:], in0=flat, in1=flat, op=MULT)
+                nc.vector.tensor_tensor(out=dest, in0=flat, in1=flat, op=MULT)
             else:
-                nc.scalar.activation(out=h_bf[e][:], in_=flat, func=ACT.Square)
+                nc.scalar.activation(out=dest, in_=flat, func=ACT.Square)
 
         def quant_h(e):
-            nc.vector.quantize_mx(out=h_words[e][:].bitcast(FP8X4), scales=h_scales[e][:], in_=h_bf[e][:])
+            nc.vector.quantize_mx(out=h_words[e][:].bitcast(FP8X4), scales=h_scales[e][:], in_=h_bf(e)[:])
 
-        def round_w2(e, q):
-            scalar_cols = W2_SCALAR[e]
-            src = w2_raw[e][q][:].rearrange("p j (b i) -> p b j i", i=4)
-            dest = w2_bf[e][q][:].rearrange("p (b i) j -> p b j i", i=4)
-            cut = scalar_cols // 4
-            if cut > 0:
-                nc.scalar.activation(out=dest[:, :cut], in_=src[:, :cut], func=ACT.Copy)
-            if scalar_cols < pieces[e][q][1]:
-                nc.vector.tensor_copy(out=dest[:, cut:], in_=src[:, cut:])
+        def round_w2(e, part, q=0):
+            w = pieces[e][q][1]
+            pool_cols = min(W2_POOL[e], w)
+            scalar_end = min(pool_cols + W2_SCALAR[e], w)
+            if part == 2 and pool_cols > 0:
+                nc.gpsimd.tensor_scalar(
+                    out=w2_bf(e, q)[:, :pool_cols, :],
+                    in0=w2_raw(e, q)[:].rearrange("p j n -> p n j")[:, :pool_cols, :],
+                    scalar1=1.0,
+                    scalar2=0.0,
+                    op0=MULT,
+                    op1=mybir.AluOpType.add,
+                )
+            src = w2_raw(e, q)[:].rearrange("p j (b i) -> p b j i", i=4)
+            dest = lambda: w2_bf(e, q)[:].rearrange("p (b i) j -> p b j i", i=4)
+            if part == 1 and scalar_end > pool_cols:
+                nc.scalar.activation(out=dest()[:, pool_cols // 4 : scalar_end // 4], in_=src[:, pool_cols // 4 : scalar_end // 4], func=ACT.Copy)
+            if part == 0 and scalar_end < w:
+                nc.vector.tensor_copy(out=dest()[:, scalar_end // 4 :], in_=src[:, scalar_end // 4 :])
 
-        def quant_w2(e, q):
+        def quant_w2(e, q=0):
             w = pieces[e][q][1]
             for a, b in ((0, min(w, 256)), (256, w)):
                 if b > a:
                     nc.vector.quantize_mx(
                         out=w2_words[e][q][:, a:b].bitcast(FP8X4),
                         scales=w2_scales[e][q][:, a:b],
-                        in_=w2_bf[e][q][:, a:b, :].rearrange("p n j -> p (n j)"),
+                        in_=w2_bf(e, q)[:, a:b, :].rearrange("p n j -> p (n j)"),
                     )
 
-        def second_layer(e, q):
+        def second_layer(e, q=0):
             n0, w = pieces[e][q]
             for c in range(w // P):
                 cols = slice(c * P, (c + 1) * P)
                 nc.tensor.matmul_mx(
-                    out=y_ps[e][q][:, c, :],
+                    out=y_ps(e, q, c),
                     lhsT=w2_words[e][q][:, cols].bitcast(FP8X4),
                     lhsT_scale=w2_scales[e][q][:, cols],
                     rhs=h_words[e][:].bitcast(FP8X4),
@@ -185,34 +236,37 @@ def tile_moe_two_mlp_relu2_kernel(tc, x_words, x_scales, w1, w2, gate, offs, dst
                     stop=True,
                 )
 
-        def apply_gate(e, q):
+        def gate_of(e):
+            if GATE4:
+                return gate_sb(e)[:]
+            s0 = (e * C) % HALF
+            return gate_sb(e // 2 * 2)[:, :, s0 : s0 + C]
+
+        def apply_gate(e, q=0):
             n0, w = pieces[e][q]
             c0 = n0 // P
-            s0 = (e * C) % HALF
-            if FUSED[e]:
-                nc.scalar.activation(out=gated[e][q][:], in_=y_ps[e][q][:], func=ACT.Copy)
-                return
-            nc.vector.tensor_tensor(
-                out=gated[e][q][:],
-                in0=y_ps[e][q][:],
-                in1=gate_sb[e * C // HALF][:, c0 : c0 + w // P, s0 : s0 + C],
-                op=MULT,
-            )
+            if YSPLIT[e] or w == P:
+                parts = [(gated(e, q)[:, c, :], y_ps(e, q, c), gate_of(e)[:, c0 + c, :]) for c in range(w // P)]
+            else:
+                parts = [(gated(e, q)[:], made[f"y{e}{q}"][:], gate_of(e))]
+            for dest, src, g in parts:
+                if FUSED[e]:
+                    nc.scalar.activation(out=dest, in_=src, func=ACT.Copy)
+                else:
+                    nc.vector.tensor_tensor(out=dest, in0=src, in1=g, op=MULT)
 
-        def scatter(e, q):
+        def scatter(e, c, q=0):
             n0, w = pieces[e][q]
             lst = dst_sb[:, e * LIST_COLS : (e + 1) * LIST_COLS]
-            for c in range(w // P):
-                window = out_sb[n0 // P + c][:].indirect(lst)
-                if FUSED[e]:
-                    s0 = (e * C) % HALF
-                    nc.vector.tensor_tensor(window, gated[e][q][:, c, :], gate_sb[e * C // HALF][:, n0 // P + c, s0 : s0 + C], MULT)
-                else:
-                    nc.vector.tensor_copy(window, gated[e][q][:, c, :])
+            window = out_sb[n0 // P + c][:].indirect(lst)
+            if FUSED[e]:
+                nc.vector.tensor_tensor(window, gated(e, q)[:, c, :], gate_of(e)[:, n0 // P + c, :], MULT)
+            else:
+                nc.vector.tensor_copy(window, gated(e, q)[:, c, :])
 
         def store(c):
             nc.sync.dma_start(out=out[c * P : (c + 1) * P, :], in_=out_sb[c][:])
 
-        stages = {"G": gather, "r": round_w1, "q": quant_w1, "f": first_layer, "h": quant_h, "R": round_w2, "Q": quant_w2, "m": second_layer, "p": apply_gate, "x": scatter, "o": store}
+        stages = {"G": gather, "r": round_w1, "q": quant_w1, "f": first_layer, "h": quant_h, "R": round_w2, "Q": quant_w2, "m": second_layer, "p": apply_gate, "x": scatter, "o": store, "u": relu, "v": square}
         for item in STEPS.split():
             stages[item[0]](*[int(ch) for ch in item[1:]])

@@ -1,6 +1,7 @@
 from contextlib import ExitStack
 
 import concourse.mybir as mybir
+from concourse.masks import make_identity
 
 K, T, E, C, H, N = 1024, 640, 4, 128, 512, 384
 
@@ -13,6 +14,7 @@ U8 = mybir.dt.uint8
 FP8X4 = mybir.dt.float8_e4m3fn_x4
 ACT = mybir.ActivationFunctionType
 MULT = mybir.AluOpType.mult
+MAX = mybir.AluOpType.max
 
 P = 128
 PACK = 4
@@ -21,35 +23,35 @@ SLOTS = E * C
 CHUNKS = N // P
 LIST_COLS = C // 16
 HALF = SLOTS // 2
-W1_SCALAR = (80, 80, 64, 80, 56, 128, 16, 80)
-W2_SCALAR = (256, 288, 32, 32)
-FUSED = (True, True, True, True)
-TAGS = {}
+W1_SCALAR = (96, 48, 32, 56, 32, 56, 32, 64)
+W2_SCALAR = (192, 0, 0, 96, 256, 0, 96, 256, 0, 32, 128, 64)
+TAGS = {'ysb10': 'w1raw210', 'w2bf11': 'relu1', 'w2bf21': 'relu2', 'ysb20': 'w1raw310', 'ysb22': 'relu3', 'ysb00': 'w1raw110'}
+RV = (2, 0, 0, 0)
+SQV = (0, 0, 0, 0)
+QSPLIT = (True, True, True, True)
+BSPLIT = (0, 1, 1, 3)
+ASPLIT = (False,) * 8
+GN = 1
+EVLATE = False
+EARLY = 0
+GSTEP = 128
+GATEV = ('000', '000', '000', '000')
+W2_POOL = (0,) * 12
+LATE2 = True
+YG = ('000', '000', '002', '012')
 SCQ = False
-QSPLIT = (True, False, False, False)
-YSPLIT = (True, True, False, False)
-RV = (1, 2, 0, 0)
-W2_POOL = (0, 0, 0, 0)
-GN = 2
-GATE4 = False
-SQUARE_V = (False, False, False, False)
-LOADS = "x f a00 s a01 b0 a10 g0 g1 d g3 b1 a11 a30 a20 a21 a31 b2 b3 g2"
-STEPS = "r210 G3 r100 r111 G1 r201 r110 R10 r000 q11 r200 r010 R01 r011 R02 r310 r301 R12 r001 r300 q00 r101 R11 q01 G0 R00 f0 q10 r211 q21 R32 R20 R31 u0 r311 f1 u1 q30 q31 v0 R21 h0 v1 G2 q20 R22 Q0 m0 Q1 f2 u2 h1 v2 p0 m1 h2 f3 x00 x02 u3 v3 Q2 p1 x12 h3 R30 Q3 m2 p2 x01 x10 m3 p3 x11 x20 x31 x30 x22 o0 x32 x21 o2 o1"
+LOADS = 'f x0 x1 s g0 a00 a01 b00 d a10 a11 b10 b11 a20 a21 b20 b21 a30 a31 b30 b31 b32'
+STEPS = ""
 
 FLOPS = 2 * SLOTS * (K * H + H * N)
 
 
 def tile_moe_two_mlp_relu2_kernel(tc, x_words, x_scales, w1, w2, gate, offs, dst, out):
     nc = tc.nc
-    last = E - 1
 
     with ExitStack() as ctx:
         keep = ctx.enter_context(tc.tile_pool(name="keep", bufs=1))
         psum = ctx.enter_context(tc.psum_pool(name="psum", bufs=1))
-
-        def sbuf(name, shape, dtype):
-            return keep.tile(shape, dtype, name=name, align_bytes=64)
-
         made = {}
 
         def buf(name, shape, dtype):
@@ -57,57 +59,64 @@ def tile_moe_two_mlp_relu2_kernel(tc, x_words, x_scales, w1, w2, gate, offs, dst
                 made[name] = keep.tile(shape, dtype, name=name, tag=TAGS.get(name, name), align_bytes=64)
             return made[name]
 
-        offs_sb = keep.tile([P, SLOTS // 16], U16, name="offs_sb")
-        dst_sb = keep.tile([P, SLOTS // 16], U16, name="dst_sb")
-        tok_words = sbuf("tok_words", [P, PASSES * T], I32)
-        tok_scales = sbuf("tok_scales", [P, T], U8)
-        slot_words = sbuf("slot_words", [P, PASSES, SLOTS], U32)
-        slot_scales = sbuf("slot_scales", [P, SLOTS], U8)
-        gate_sb = lambda u: buf(f"gate{u}", [P, CHUNKS, C if GATE4 else HALF], F32)
-        out_sb = [sbuf(f"out{c}", [P, T], F32) for c in range(CHUNKS)]
-
-        w1_raw = lambda e, o: buf(f"w1raw{e}{o}", [P, PACK, H], F32)
-        w1_bf = lambda e, o: buf(f"w1bf{e}{o}", [P, PACK, P, PACK], BF16)
-        w1_words = [[sbuf(f"w1w{e}_{o}", [P, H], U32) for o in range(PASSES)] for e in range(E)]
-        w1_scales = [[sbuf(f"w1s{e}_{o}", [P, H], U8) for o in range(PASSES)] for e in range(E)]
-        pieces = [[(0, N)] for e in range(E)]
-        w2_raw = lambda e, q: buf(f"w2raw{e}{q}", [P, PACK, pieces[e][q][1]], F32)
-        w2_bf = lambda e, q: buf(f"w2bf{e}{q}", [P, pieces[e][q][1], PACK], BF16)
-        w2_words = [[sbuf(f"w2w{e}_{n0}", [P, w], U32) for n0, w in pieces[e]] for e in range(E)]
-        w2_scales = [[sbuf(f"w2s{e}_{n0}", [P, w], U8) for n0, w in pieces[e]] for e in range(E)]
-        relu_sb = lambda e: buf(f"relu{e}", [P, PACK, C], F32)
-        h_bf = lambda e: buf(f"hbf{e}", [P, C * PACK], BF16)
-        h_words = [sbuf(f"hw{e}", [P, C], U32) for e in range(E)]
-        h_scales = [sbuf(f"hs{e}", [P, C], U8) for e in range(E)]
-        gated = lambda e, q: buf(f"gated{e}{q}", [P, pieces[e][q][1] // P, C], F32)
         def bank(name, tag, shape):
             if name not in made:
-                made[name] = psum.tile(shape, F32, name=name, tag=tag)
+                made[name] = psum.tile(shape, F32, name=name, tag=TAGS.get(name, tag))
             return made[name]
 
-        a_ps = lambda e, t: bank(f"a{e}{t}", f"a{t}", [P, C])
+        offs_sb = keep.tile([P, SLOTS // 16], U16, name="offs_sb")
+        dst_sb = keep.tile([P, SLOTS // 16], U16, name="dst_sb")
+        tok_words = [buf(f"tok_words{o}", [P, T], I32) for o in range(PASSES)]
+        tok_scales = buf("tok_scales", [P, T], U8)
+        slot_words = [buf(f"slot_words{o}", [P, SLOTS], U32) for o in range(PASSES)]
+        slot_scales = buf("slot_scales", [P, SLOTS], U8)
+        gate_col = buf("gate_col", [P, PACK], F32)
+        ident = buf("ident", [P, P], F32)
+        out_sb = [buf(f"out{c}", [P, T], F32) for c in range(CHUNKS)]
+        cuts = {0: [(0, N)], 1: [(0, P), (P, 2 * P)], 2: [(0, 2 * P), (2 * P, P)], 3: [(c * P, P) for c in range(CHUNKS)]}
+        pieces = [cuts[BSPLIT[e]] for e in range(E)]
+        halves = lambda e, o: 2 if ASPLIT[e * PASSES + o] else 1
+        gw = SLOTS // GN
 
-        def y_ps(e, q, c):
-            n0, w = pieces[e][q]
-            if YSPLIT[e] or w == P:
-                return bank(f"y{e}{q}{c}", f"y{n0 // P + c}", [P, C])[:]
-            return bank(f"y{e}{q}", f"y{3 - e % 2}", [P, w // P, C])[:, c, :]
+        gate_sb = lambda u: buf(f"gate{u}", [P, gw], F32)
+        w1_raw = lambda e, o, u: buf(f"w1raw{e}{o}{u}", [P, PACK, H // halves(e, o)], F32)
+        w1_bf = lambda e, o: buf(f"w1bf{e}{o}", [P, PACK, P, PACK], BF16)
+        w1_words = lambda e, o: buf(f"w1w{e}{o}", [P, H], U32)
+        w1_scales = lambda e, o: buf(f"w1s{e}{o}", [P, H], U8)
+        w2_raw = lambda e, q: buf(f"w2raw{e}{q}", [P, PACK, pieces[e][q][1]], F32)
+        w2_bf = lambda e, q: buf(f"w2bf{e}{q}", [P, pieces[e][q][1], PACK], BF16)
+        w2_words = lambda e: buf(f"w2w{e}", [P, N], U32)
+        w2_scales = lambda e: buf(f"w2s{e}", [P, N], U8)
+        relu_sb = lambda e: buf(f"relu{e}", [P, PACK, C], F32)
+        h_bf = lambda e: buf(f"hbf{e}", [P, C * PACK], BF16)
+        h_words = lambda e: buf(f"hw{e}", [P, C], U32)
+        h_scales = lambda e: buf(f"hs{e}", [P, C], U8)
+        y_sb = lambda e, c: buf(f"ysb{e}{YG[e][c]}", [P, CHUNKS, C], F32)[:, c, :]
+        a_ps = lambda e, t: bank(f"a{e}{t}", f"a{t}", [P, C])
+        y_ps = lambda e, c: bank(f"y{e}{c}", f"y{c}", [P, C])
 
         def load_w1(e, o):
-            rows = w1[e, o * P * PACK : (o + 1) * P * PACK, :]
-            nc.sync.dma_start(out=w1_raw(e, o)[:], in_=rows.rearrange("(p j) i -> p j i", j=PACK))
+            w = H // halves(e, o)
+            for u in range(halves(e, o)):
+                rows = w1[e, o * P * PACK : (o + 1) * P * PACK, u * w : (u + 1) * w]
+                nc.sync.dma_start(out=w1_raw(e, o, u)[:], in_=rows.rearrange("(p j) i -> p j i", j=PACK))
 
         def load_w2(e, q=0):
-            n0, w = pieces[e][q]
-            nc.sync.dma_start(out=w2_raw(e, q)[:], in_=w2[e, :, n0 : n0 + w].rearrange("(p j) n -> p j n", j=PACK))
+            if q < len(pieces[e]):
+                n0, w = pieces[e][q]
+                nc.sync.dma_start(out=w2_raw(e, q)[:], in_=w2[e, :, n0 : n0 + w].rearrange("(p j) n -> p j n", j=PACK))
 
         def load_gate(u):
-            if not GATE4 and u % 2:
-                return
-            cols = gate[:, u * C : u * C + (C if GATE4 else HALF)]
-            nc.sync.dma_start(out=gate_sb(u)[:], in_=cols.rearrange("(c p) s -> p c s", p=P))
+            nc.sync.dma_start(out=gate_col[:], in_=gate[0, :].rearrange("(p j) -> p j", j=PACK))
+
+        def spread_gate():
+            ps = bank("gate_ps", "gate_ps", [P, PACK, P])
+            for j in range(PACK):
+                nc.tensor.transpose(ps[:, j, :], gate_col[:, j : j + 1].to_broadcast([P, P]), ident[:])
+            nc.scalar.copy(out=gate_sb(0)[:].rearrange("p (s j) -> p s j", j=PACK), in_=ps[:].rearrange("p j s -> p s j"))
 
         nc.vector.memset(tok_scales[:].bitcast(I32), 0)
+        make_identity(nc, ident[:])
         for c in range(CHUNKS):
             nc.gpsimd.memset(out_sb[c][:], 0.0)
 
@@ -118,155 +127,167 @@ def tile_moe_two_mlp_relu2_kernel(tc, x_words, x_scales, w1, w2, gate, offs, dst
                     in_=x_scales[:, 4 * q : 4 * q + 4, :].bitcast(I32),
                 )
 
-        def load_x():
-            nc.sync.dma_start(
-                out=tok_words[:].rearrange("p (o t) -> p o t", o=PASSES),
-                in_=x_words.rearrange("o p t r -> p o (t r)").bitcast(I32),
-            )
+        def load_x(o):
+            nc.sync.dma_start(out=tok_words[o][:], in_=x_words[o].rearrange("p t r -> p (t r)").bitcast(I32))
 
         loaders = {"a": load_w1, "b": load_w2, "g": load_gate, "s": load_scales, "x": load_x, "f": lambda: nc.sync.dma_start(offs_sb[:], offs), "d": lambda: nc.sync.dma_start(dst_sb[:], dst)}
         for item in LOADS.split():
             loaders[item[0]](*[int(ch) for ch in item[1:]])
 
         def gather(u):
-            if GN == 2 and u % 2:
-                return
-            width = SLOTS // GN
-            cols = slice(u * C, u * C + width)
-            lst = offs_sb[:, u * C // 16 : (u * C + width) // 16]
+            cols = slice(u * HALF, (u + 1) * HALF)
+            lst = offs_sb[:, u * HALF // 16 : (u + 1) * HALF // 16]
             for o in range(PASSES):
-                window = tok_words[:, o * T : (o + 1) * T].bitcast(U32)
-                nc.vector.tensor_copy(slot_words[:, o, cols], window.indirect(lst))
+                nc.vector.tensor_copy(slot_words[o][:, cols], tok_words[o][:].bitcast(U32).indirect(lst))
             nc.vector.tensor_copy(slot_scales[:, cols], tok_scales[:].indirect(lst))
 
-        def round_w1(e, o, on_scalar):
-            src = w1_raw(e, o)[:].rearrange("p j (m t) -> p m j t", t=PACK)
-            cut = W1_SCALAR[e * PASSES + o]
-            if on_scalar and cut > 0:
-                dest = w1_bf(e, o)[:].rearrange("p t m j -> p m j t")
-                nc.scalar.activation(out=dest[:, :cut], in_=src[:, :cut], func=ACT.Copy)
-            if not on_scalar and cut < P:
-                dest = w1_bf(e, o)[:].rearrange("p t m j -> p m j t")
-                nc.vector.tensor_copy(out=dest[:, cut:], in_=src[:, cut:])
+        def round_w1(e, o):
+            n = halves(e, o)
+            w = P // n
+            for u in range(n):
+                src = w1_raw(e, o, u)[:].rearrange("p j (m t) -> p m j t", t=PACK)
+                dest = w1_bf(e, o)[:].rearrange("p t m j -> p m j t")[:, u * w : (u + 1) * w]
+                cut = W1_SCALAR[e * PASSES + o] // n // 2 * 2
+                if cut > 0:
+                    nc.scalar.activation(out=dest[:, :cut], in_=src[:, :cut], func=ACT.Copy)
+                if cut < w:
+                    nc.vector.tensor_copy(out=dest[:, cut:], in_=src[:, cut:])
 
         def quant_w1(e, o):
             step = P if (QSPLIT[e] and o == PASSES - 1) else H
             flat = w1_bf(e, o)[:].rearrange("p t m j -> p (t m j)")
             for a in range(0, H, step):
                 nc.vector.quantize_mx(
-                    out=w1_words[e][o][:, a : a + step].bitcast(FP8X4),
-                    scales=w1_scales[e][o][:, a : a + step],
+                    out=w1_words(e, o)[:, a : a + step].bitcast(FP8X4),
+                    scales=w1_scales(e, o)[:, a : a + step],
                     in_=flat[:, a * PACK : (a + step) * PACK],
                 )
 
-        def first_layer(e):
+        def first_layer(e, o):
             slots = slice(e * C, (e + 1) * C)
-            for o in range(PASSES):
-                for t in range(PACK):
-                    cols = slice(t * P, (t + 1) * P)
-                    nc.tensor.matmul_mx(
-                        out=a_ps(e, t)[:],
-                        lhsT=w1_words[e][o][:, cols].bitcast(FP8X4),
-                        lhsT_scale=w1_scales[e][o][:, cols],
-                        rhs=slot_words[:, o, slots].bitcast(FP8X4),
-                        rhs_scale=slot_scales[4 * o :, slots],
-                        start=(o == 0),
-                        stop=(o == PASSES - 1),
-                    )
+            for t in range(PACK):
+                cols = slice(t * P, (t + 1) * P)
+                nc.tensor.matmul_mx(
+                    out=a_ps(e, t)[:],
+                    lhsT=w1_words(e, o)[:, cols].bitcast(FP8X4),
+                    lhsT_scale=w1_scales(e, o)[:, cols],
+                    rhs=slot_words[o][:, slots].bitcast(FP8X4),
+                    rhs_scale=slot_scales[4 * o :, slots],
+                    start=(o == 0),
+                    stop=(o == PASSES - 1),
+                )
 
         def relu(e):
             for t in range(PACK):
                 if t >= PACK - RV[e]:
-                    nc.vector.tensor_scalar(out=relu_sb(e)[:, t, :], in0=a_ps(e, t)[:], scalar1=0.0, scalar2=None, op0=mybir.AluOpType.max)
+                    nc.vector.tensor_scalar(out=relu_sb(e)[:, t, :], in0=a_ps(e, t)[:], scalar1=0.0, scalar2=None, op0=MAX)
                 else:
                     nc.scalar.activation(out=relu_sb(e)[:, t, :], in_=a_ps(e, t)[:], func=ACT.Relu)
 
         def square(e):
             flat = relu_sb(e)[:].rearrange("p t s -> p s t")
             dest = h_bf(e)[:].rearrange("p (s t) -> p s t", t=PACK)
-            if SQUARE_V[e]:
-                nc.vector.tensor_tensor(out=dest, in0=flat, in1=flat, op=MULT)
-            else:
-                nc.scalar.activation(out=dest, in_=flat, func=ACT.Square)
+            cut = C - SQV[e]
+            if cut > 0:
+                nc.scalar.activation(out=dest[:, :cut], in_=flat[:, :cut], func=ACT.Square)
+            if cut < C:
+                nc.vector.tensor_tensor(out=dest[:, cut:], in0=flat[:, cut:], in1=flat[:, cut:], op=MULT)
 
         def quant_h(e):
-            nc.vector.quantize_mx(out=h_words[e][:].bitcast(FP8X4), scales=h_scales[e][:], in_=h_bf(e)[:])
+            nc.vector.quantize_mx(out=h_words(e)[:].bitcast(FP8X4), scales=h_scales(e)[:], in_=h_bf(e)[:])
 
-        def round_w2(e, part, q=0):
+        def round_w2(e, q):
             w = pieces[e][q][1]
-            pool_cols = min(W2_POOL[e], w)
-            scalar_end = min(pool_cols + W2_SCALAR[e], w)
-            if part == 2 and pool_cols > 0:
+            pool = min(W2_POOL[e * 3 + q], w)
+            for a in range(0, pool, GSTEP):
+                b = min(a + GSTEP, pool)
                 nc.gpsimd.tensor_scalar(
-                    out=w2_bf(e, q)[:, :pool_cols, :],
-                    in0=w2_raw(e, q)[:].rearrange("p j n -> p n j")[:, :pool_cols, :],
+                    out=w2_bf(e, q)[:, a:b, :],
+                    in0=w2_raw(e, q)[:].rearrange("p j n -> p n j")[:, a:b, :],
                     scalar1=1.0,
                     scalar2=0.0,
                     op0=MULT,
                     op1=mybir.AluOpType.add,
                 )
+            lo = pool // 4
+            cut = min(pool + W2_SCALAR[e * 3 + q], w) // 8 * 2
             src = w2_raw(e, q)[:].rearrange("p j (b i) -> p b j i", i=4)
-            dest = lambda: w2_bf(e, q)[:].rearrange("p (b i) j -> p b j i", i=4)
-            if part == 1 and scalar_end > pool_cols:
-                nc.scalar.activation(out=dest()[:, pool_cols // 4 : scalar_end // 4], in_=src[:, pool_cols // 4 : scalar_end // 4], func=ACT.Copy)
-            if part == 0 and scalar_end < w:
-                nc.vector.tensor_copy(out=dest()[:, scalar_end // 4 :], in_=src[:, scalar_end // 4 :])
+            dest = w2_bf(e, q)[:].rearrange("p (b i) j -> p b j i", i=4)
+            if cut > lo:
+                nc.scalar.activation(out=dest[:, lo:cut], in_=src[:, lo:cut], func=ACT.Copy)
+            if cut < w // 4:
+                nc.vector.tensor_copy(out=dest[:, cut:], in_=src[:, cut:])
 
-        def quant_w2(e, q=0):
-            w = pieces[e][q][1]
+        def quant_w2(e, q):
+            n0, w = pieces[e][q]
             for a, b in ((0, min(w, 256)), (256, w)):
                 if b > a:
                     nc.vector.quantize_mx(
-                        out=w2_words[e][q][:, a:b].bitcast(FP8X4),
-                        scales=w2_scales[e][q][:, a:b],
+                        out=w2_words(e)[:, n0 + a : n0 + b].bitcast(FP8X4),
+                        scales=w2_scales(e)[:, n0 + a : n0 + b],
                         in_=w2_bf(e, q)[:, a:b, :].rearrange("p n j -> p (n j)"),
                     )
 
-        def second_layer(e, q=0):
-            n0, w = pieces[e][q]
-            for c in range(w // P):
-                cols = slice(c * P, (c + 1) * P)
-                nc.tensor.matmul_mx(
-                    out=y_ps(e, q, c),
-                    lhsT=w2_words[e][q][:, cols].bitcast(FP8X4),
-                    lhsT_scale=w2_scales[e][q][:, cols],
-                    rhs=h_words[e][:].bitcast(FP8X4),
-                    rhs_scale=h_scales[e][:],
-                    start=True,
-                    stop=True,
-                )
+        def second_layer(e, c):
+            cols = slice(c * P, (c + 1) * P)
+            nc.tensor.matmul_mx(
+                out=y_ps(e, c)[:],
+                lhsT=w2_words(e)[:, cols].bitcast(FP8X4),
+                lhsT_scale=w2_scales(e)[:, cols],
+                rhs=h_words(e)[:].bitcast(FP8X4),
+                rhs_scale=h_scales(e)[:],
+                start=True,
+                stop=True,
+            )
 
         def gate_of(e):
-            if GATE4:
-                return gate_sb(e)[:]
-            s0 = (e * C) % HALF
-            return gate_sb(e // 2 * 2)[:, :, s0 : s0 + C]
+            return gate_sb(e * C // gw)[:, e * C % gw : e * C % gw + C]
 
-        def apply_gate(e, q=0):
-            n0, w = pieces[e][q]
-            c0 = n0 // P
-            if YSPLIT[e] or w == P:
-                parts = [(gated(e, q)[:, c, :], y_ps(e, q, c), gate_of(e)[:, c0 + c, :]) for c in range(w // P)]
+        def evacuate(e, c):
+            if GATEV[e][c] == "1":
+                nc.vector.tensor_tensor(out=y_sb(e, c)[:], in0=y_ps(e, c)[:], in1=gate_of(e), op=MULT)
             else:
-                parts = [(gated(e, q)[:], made[f"y{e}{q}"][:], gate_of(e))]
-            for dest, src, g in parts:
-                if FUSED[e]:
-                    nc.scalar.activation(out=dest, in_=src, func=ACT.Copy)
-                else:
-                    nc.vector.tensor_tensor(out=dest, in0=src, in1=g, op=MULT)
+                nc.scalar.activation(out=y_sb(e, c)[:], in_=y_ps(e, c)[:], func=ACT.Copy)
 
-        def scatter(e, c, q=0):
-            n0, w = pieces[e][q]
+        def scatter(e, c):
             lst = dst_sb[:, e * LIST_COLS : (e + 1) * LIST_COLS]
-            window = out_sb[n0 // P + c][:].indirect(lst)
-            if FUSED[e]:
-                nc.vector.tensor_tensor(window, gated(e, q)[:, c, :], gate_of(e)[:, n0 // P + c, :], MULT)
+            if GATEV[e][c] == "1":
+                nc.vector.tensor_copy(out_sb[c][:].indirect(lst), y_sb(e, c)[:])
             else:
-                nc.vector.tensor_copy(window, gated(e, q)[:, c, :])
+                nc.vector.tensor_tensor(out_sb[c][:].indirect(lst), y_sb(e, c)[:], gate_of(e), MULT)
 
         def store(c):
             nc.sync.dma_start(out=out[c * P : (c + 1) * P, :], in_=out_sb[c][:])
 
-        stages = {"G": gather, "r": round_w1, "q": quant_w1, "f": first_layer, "h": quant_h, "R": round_w2, "Q": quant_w2, "m": second_layer, "p": apply_gate, "x": scatter, "o": store, "u": relu, "v": square}
-        for item in STEPS.split():
-            stages[item[0]](*[int(ch) for ch in item[1:]])
+        spread_gate()
+        gather(0)
+        for e in range(E):
+            for o in range(PASSES):
+                round_w1(e, o)
+                quant_w1(e, o)
+                first_layer(e, o)
+            if e > 0 and not EVLATE:
+                for c in range(EARLY, CHUNKS - (e == E - 1 and LATE2)):
+                    evacuate(e - 1, c)
+            relu(e)
+            square(e)
+            quant_h(e)
+            if e == E - 1 and LATE2:
+                evacuate(e - 1, CHUNKS - 1)
+            for q in range(len(pieces[e])):
+                round_w2(e, q)
+                quant_w2(e, q)
+            if e > 0 and EVLATE:
+                for c in range(CHUNKS):
+                    evacuate(e - 1, c)
+            for c in range(CHUNKS):
+                second_layer(e, c)
+                if c < EARLY or e == E - 1:
+                    evacuate(e, c)
+            if e == 0:
+                gather(1)
+        for e in range(E):
+            for c in range(CHUNKS):
+                scatter(e, c)
+        for c in range(CHUNKS):
+            store(c)

@@ -14,34 +14,20 @@ U8 = mybir.dt.uint8
 FP8X4 = mybir.dt.float8_e4m3fn_x4
 ACT = mybir.ActivationFunctionType
 MULT = mybir.AluOpType.mult
-MAX = mybir.AluOpType.max
 
 P = 128
 PACK = 4
 PASSES = K // (P * PACK)
 SLOTS = E * C
 CHUNKS = N // P
-LIST_COLS = C // 16
+PER_COL = 16
+QUADRANT = 32
 HALF = SLOTS // 2
-W1_SCALAR = (96, 48, 32, 56, 32, 56, 32, 64)
-W2_SCALAR = (192, 0, 0, 96, 256, 0, 96, 256, 0, 32, 128, 64)
-TAGS = {'ysb10': 'w1raw210', 'w2bf11': 'relu1', 'w2bf21': 'relu2', 'ysb20': 'w1raw310', 'ysb22': 'relu3', 'ysb00': 'w1raw110'}
-RV = (2, 0, 0, 0)
-SQV = (0, 0, 0, 0)
-QSPLIT = (True, True, True, True)
-BSPLIT = (0, 1, 1, 3)
-ASPLIT = (False,) * 8
-GN = 1
-EVLATE = False
-EARLY = 0
-GSTEP = 128
-GATEV = ('000', '000', '000', '000')
-W2_POOL = (0,) * 12
-LATE2 = True
-YG = ('000', '000', '002', '012')
-SCQ = False
-LOADS = 'f x0 x1 s g0 a00 a01 b00 d a10 a11 b10 b11 a20 a21 b20 b21 a30 a31 b30 b31 b32'
-STEPS = ""
+LAST = E - 1
+
+W1_ON_SCALAR = (48, 72)
+LAST_PASS_ON_SCALAR = 80
+LAST_CHUNK1_ON_SCALAR = 32
 
 FLOPS = 2 * SLOTS * (K * H + H * N)
 
@@ -52,242 +38,188 @@ def tile_moe_two_mlp_relu2_kernel(tc, x_words, x_scales, w1, w2, gate, offs, dst
     with ExitStack() as ctx:
         keep = ctx.enter_context(tc.tile_pool(name="keep", bufs=1))
         psum = ctx.enter_context(tc.psum_pool(name="psum", bufs=1))
-        made = {}
 
-        def buf(name, shape, dtype):
-            if name not in made:
-                made[name] = keep.tile(shape, dtype, name=name, tag=TAGS.get(name, name), align_bytes=64)
-            return made[name]
+        def sbuf(name, shape, dtype, tag=None):
+            return keep.tile(shape, dtype, name=name, tag=tag or name, align_bytes=64)
 
-        def bank(name, tag, shape):
-            if name not in made:
-                made[name] = psum.tile(shape, F32, name=name, tag=TAGS.get(name, tag))
-            return made[name]
-
-        offs_sb = keep.tile([P, SLOTS // 16], U16, name="offs_sb")
-        dst_sb = keep.tile([P, SLOTS // 16], U16, name="dst_sb")
-        tok_words = [buf(f"tok_words{o}", [P, T], I32) for o in range(PASSES)]
-        tok_scales = buf("tok_scales", [P, T], U8)
-        slot_words = [buf(f"slot_words{o}", [P, SLOTS], U32) for o in range(PASSES)]
-        slot_scales = buf("slot_scales", [P, SLOTS], U8)
-        gate_col = buf("gate_col", [P, PACK], F32)
-        ident = buf("ident", [P, P], F32)
-        out_sb = [buf(f"out{c}", [P, T], F32) for c in range(CHUNKS)]
-        cuts = {0: [(0, N)], 1: [(0, P), (P, 2 * P)], 2: [(0, 2 * P), (2 * P, P)], 3: [(c * P, P) for c in range(CHUNKS)]}
-        pieces = [cuts[BSPLIT[e]] for e in range(E)]
-        halves = lambda e, o: 2 if ASPLIT[e * PASSES + o] else 1
-        gw = SLOTS // GN
-
-        gate_sb = lambda u: buf(f"gate{u}", [P, gw], F32)
-        w1_raw = lambda e, o, u: buf(f"w1raw{e}{o}{u}", [P, PACK, H // halves(e, o)], F32)
-        w1_bf = lambda e, o: buf(f"w1bf{e}{o}", [P, PACK, P, PACK], BF16)
-        w1_words = lambda e, o: buf(f"w1w{e}{o}", [P, H], U32)
-        w1_scales = lambda e, o: buf(f"w1s{e}{o}", [P, H], U8)
-        w2_raw = lambda e, q: buf(f"w2raw{e}{q}", [P, PACK, pieces[e][q][1]], F32)
-        w2_bf = lambda e, q: buf(f"w2bf{e}{q}", [P, pieces[e][q][1], PACK], BF16)
-        w2_words = lambda e: buf(f"w2w{e}", [P, N], U32)
-        w2_scales = lambda e: buf(f"w2s{e}", [P, N], U8)
-        relu_sb = lambda e: buf(f"relu{e}", [P, PACK, C], F32)
-        h_bf = lambda e: buf(f"hbf{e}", [P, C * PACK], BF16)
-        h_words = lambda e: buf(f"hw{e}", [P, C], U32)
-        h_scales = lambda e: buf(f"hs{e}", [P, C], U8)
-        y_sb = lambda e, c: buf(f"ysb{e}{YG[e][c]}", [P, CHUNKS, C], F32)[:, c, :]
-        a_ps = lambda e, t: bank(f"a{e}{t}", f"a{t}", [P, C])
-        y_ps = lambda e, c: bank(f"y{e}{c}", f"y{c}", [P, C])
-
-        def load_w1(e, o):
-            w = H // halves(e, o)
-            for u in range(halves(e, o)):
-                rows = w1[e, o * P * PACK : (o + 1) * P * PACK, u * w : (u + 1) * w]
-                nc.sync.dma_start(out=w1_raw(e, o, u)[:], in_=rows.rearrange("(p j) i -> p j i", j=PACK))
-
-        def load_w2(e, q=0):
-            if q < len(pieces[e]):
-                n0, w = pieces[e][q]
-                nc.sync.dma_start(out=w2_raw(e, q)[:], in_=w2[e, :, n0 : n0 + w].rearrange("(p j) n -> p j n", j=PACK))
-
-        def load_gate(u):
-            nc.sync.dma_start(out=gate_col[:], in_=gate[0, :].rearrange("(p j) -> p j", j=PACK))
-
-        def spread_gate():
-            ps = bank("gate_ps", "gate_ps", [P, PACK, P])
-            for j in range(PACK):
-                nc.tensor.transpose(ps[:, j, :], gate_col[:, j : j + 1].to_broadcast([P, P]), ident[:])
-            nc.scalar.copy(out=gate_sb(0)[:].rearrange("p (s j) -> p s j", j=PACK), in_=ps[:].rearrange("p j s -> p s j"))
+        offs_sb = keep.tile([P, SLOTS // PER_COL], U16, name="offs_sb")
+        dst_sb = keep.tile([P, SLOTS // PER_COL], U16, name="dst_sb")
+        tok_words = sbuf("tok_words", [P, PASSES * T], I32)
+        tok_scales = sbuf("tok_scales", [P, T], U8)
+        slot_words = [sbuf(f"slot_words{o}", [P, SLOTS], U32) for o in range(PASSES)]
+        slot_scales = sbuf("slot_scales", [P, SLOTS], U8)
+        gate_row = sbuf("gate_row", [P, PACK], F32)
+        gate_sb = sbuf("gate_sb", [P, SLOTS], F32)
+        ident = sbuf("ident", [P, P], F32)
+        out_sb = [sbuf(f"out{c}", [P, T], F32) for c in range(CHUNKS)]
 
         nc.vector.memset(tok_scales[:].bitcast(I32), 0)
         make_identity(nc, ident[:])
         for c in range(CHUNKS):
             nc.gpsimd.memset(out_sb[c][:], 0.0)
 
-        def load_scales():
-            for q in range(4):
-                (nc.scalar if SCQ else nc.sync).dma_start(
-                    out=tok_scales[32 * q : 32 * q + 4 * PASSES, :].bitcast(I32),
-                    in_=x_scales[:, 4 * q : 4 * q + 4, :].bitcast(I32),
-                )
+        w1_raw = {}
+        w2_raw = {}
 
-        def load_x(o):
-            nc.sync.dma_start(out=tok_words[o][:], in_=x_words[o].rearrange("p t r -> p (t r)").bitcast(I32))
+        def load_w1(e, o):
+            w1_raw[e, o] = sbuf(f"w1raw{e}{o}", [P, PACK, H], F32)
+            rows = w1[e, o * P * PACK : (o + 1) * P * PACK, :]
+            nc.sync.dma_start(out=w1_raw[e, o][:], in_=rows.rearrange("(p j) i -> p j i", j=PACK))
 
-        loaders = {"a": load_w1, "b": load_w2, "g": load_gate, "s": load_scales, "x": load_x, "f": lambda: nc.sync.dma_start(offs_sb[:], offs), "d": lambda: nc.sync.dma_start(dst_sb[:], dst)}
-        for item in LOADS.split():
-            loaders[item[0]](*[int(ch) for ch in item[1:]])
+        def load_w2(e):
+            w2_raw[e] = sbuf(f"w2raw{e}", [P, PACK, N], F32)
+            nc.sync.dma_start(out=w2_raw[e][:], in_=w2[e].rearrange("(p j) n -> p j n", j=PACK))
 
-        def gather(u):
-            cols = slice(u * HALF, (u + 1) * HALF)
-            lst = offs_sb[:, u * HALF // 16 : (u + 1) * HALF // 16]
+        nc.sync.dma_start(offs_sb[:], offs)
+        nc.sync.dma_start(
+            out=tok_words[:].rearrange("p (o t) -> p o t", o=PASSES),
+            in_=x_words.rearrange("o p t r -> p o (t r)").bitcast(I32),
+        )
+        load_w1(0, 0)
+        for q in range(P // QUADRANT):
+            nc.sync.dma_start(
+                out=tok_scales[QUADRANT * q : QUADRANT * q + 4 * PASSES, :].bitcast(I32),
+                in_=x_scales[:, 4 * q : 4 * q + 4, :].bitcast(I32),
+            )
+        nc.sync.dma_start(out=gate_row[:], in_=gate[0, :].rearrange("(p j) -> p j", j=PACK))
+        load_w1(0, 1)
+        load_w2(0)
+        nc.sync.dma_start(dst_sb[:], dst)
+        for e in range(1, E):
+            load_w1(e, 0)
+            load_w1(e, 1)
+            load_w2(e)
+
+        def spread_gate():
+            spread = psum.tile([P, PACK, P], F32, name="gate_ps")
+            for j in range(PACK):
+                nc.tensor.transpose(spread[:, j, :], gate_row[:, j : j + 1].to_broadcast([P, P]), ident[:])
+            nc.scalar.copy(out=gate_sb[:].rearrange("p (s j) -> p s j", j=PACK), in_=spread[:].rearrange("p j s -> p s j"))
+
+        def gather(half):
+            cols = slice(half * HALF, (half + 1) * HALF)
+            entries = offs_sb[:, half * HALF // PER_COL : (half + 1) * HALF // PER_COL]
             for o in range(PASSES):
-                nc.vector.tensor_copy(slot_words[o][:, cols], tok_words[o][:].bitcast(U32).indirect(lst))
-            nc.vector.tensor_copy(slot_scales[:, cols], tok_scales[:].indirect(lst))
+                window = tok_words[:, o * T : (o + 1) * T].bitcast(U32)
+                nc.vector.tensor_copy(slot_words[o][:, cols], window.indirect(entries))
+            nc.vector.tensor_copy(slot_scales[:, cols], tok_scales[:].indirect(entries))
 
-        def round_w1(e, o):
-            n = halves(e, o)
-            w = P // n
-            for u in range(n):
-                src = w1_raw(e, o, u)[:].rearrange("p j (m t) -> p m j t", t=PACK)
-                dest = w1_bf(e, o)[:].rearrange("p t m j -> p m j t")[:, u * w : (u + 1) * w]
-                cut = W1_SCALAR[e * PASSES + o] // n // 2 * 2
-                if cut > 0:
-                    nc.scalar.activation(out=dest[:, :cut], in_=src[:, :cut], func=ACT.Copy)
-                if cut < w:
-                    nc.vector.tensor_copy(out=dest[:, cut:], in_=src[:, cut:])
+        def first_layer_pass(e, o, banks):
+            rounded = sbuf(f"w1bf{e}{o}", [P, PACK, P, PACK], BF16)
+            src = w1_raw[e, o][:].rearrange("p j (m t) -> p m j t", t=PACK)
+            dest = rounded[:].rearrange("p t m j -> p m j t")
+            cut = LAST_PASS_ON_SCALAR if (e, o) == (LAST, PASSES - 1) else W1_ON_SCALAR[o]
+            nc.scalar.copy(out=dest[:, :cut], in_=src[:, :cut])
+            nc.vector.tensor_copy(out=dest[:, cut:], in_=src[:, cut:])
 
-        def quant_w1(e, o):
-            step = P if (QSPLIT[e] and o == PASSES - 1) else H
-            flat = w1_bf(e, o)[:].rearrange("p t m j -> p (t m j)")
+            words = sbuf(f"w1w{e}{o}", [P, H], U32)
+            scales = sbuf(f"w1s{e}{o}", [P, H], U8)
+            flat = rounded[:].rearrange("p t m j -> p (t m j)")
+            step = P if o == PASSES - 1 else H
             for a in range(0, H, step):
                 nc.vector.quantize_mx(
-                    out=w1_words(e, o)[:, a : a + step].bitcast(FP8X4),
-                    scales=w1_scales(e, o)[:, a : a + step],
+                    out=words[:, a : a + step].bitcast(FP8X4),
+                    scales=scales[:, a : a + step],
                     in_=flat[:, a * PACK : (a + step) * PACK],
                 )
 
-        def first_layer(e, o):
             slots = slice(e * C, (e + 1) * C)
             for t in range(PACK):
                 cols = slice(t * P, (t + 1) * P)
                 nc.tensor.matmul_mx(
-                    out=a_ps(e, t)[:],
-                    lhsT=w1_words(e, o)[:, cols].bitcast(FP8X4),
-                    lhsT_scale=w1_scales(e, o)[:, cols],
+                    out=banks[t][:],
+                    lhsT=words[:, cols].bitcast(FP8X4),
+                    lhsT_scale=scales[:, cols],
                     rhs=slot_words[o][:, slots].bitcast(FP8X4),
                     rhs_scale=slot_scales[4 * o :, slots],
                     start=(o == 0),
                     stop=(o == PASSES - 1),
                 )
 
-        def relu(e):
-            for t in range(PACK):
-                if t >= PACK - RV[e]:
-                    nc.vector.tensor_scalar(out=relu_sb(e)[:, t, :], in0=a_ps(e, t)[:], scalar1=0.0, scalar2=None, op0=MAX)
-                else:
-                    nc.scalar.activation(out=relu_sb(e)[:, t, :], in_=a_ps(e, t)[:], func=ACT.Relu)
+        def round_w2(copy, e, first, dest):
+            src = w2_raw[e][:, :, first : first + dest.shape[1]]
+            copy(out=dest.rearrange("p (b u) j -> p b j u", u=4), in_=src.rearrange("p j (b u) -> p b j u", u=4))
 
-        def square(e):
-            flat = relu_sb(e)[:].rearrange("p t s -> p s t")
-            dest = h_bf(e)[:].rearrange("p (s t) -> p s t", t=PACK)
-            cut = C - SQV[e]
-            if cut > 0:
-                nc.scalar.activation(out=dest[:, :cut], in_=flat[:, :cut], func=ACT.Square)
-            if cut < C:
-                nc.vector.tensor_tensor(out=dest[:, cut:], in0=flat[:, cut:], in1=flat[:, cut:], op=MULT)
+        def quantise(mx, rounded, first, end):
+            words, scales = mx
+            nc.vector.quantize_mx(
+                out=words[:, first:end].bitcast(FP8X4),
+                scales=scales[:, first:end],
+                in_=rounded[:, first:end, :].rearrange("p n j -> p (n j)"),
+            )
 
-        def quant_h(e):
-            nc.vector.quantize_mx(out=h_words(e)[:].bitcast(FP8X4), scales=h_scales(e)[:], in_=h_bf(e)[:])
-
-        def round_w2(e, q):
-            w = pieces[e][q][1]
-            pool = min(W2_POOL[e * 3 + q], w)
-            for a in range(0, pool, GSTEP):
-                b = min(a + GSTEP, pool)
-                nc.gpsimd.tensor_scalar(
-                    out=w2_bf(e, q)[:, a:b, :],
-                    in0=w2_raw(e, q)[:].rearrange("p j n -> p n j")[:, a:b, :],
-                    scalar1=1.0,
-                    scalar2=0.0,
-                    op0=MULT,
-                    op1=mybir.AluOpType.add,
-                )
-            lo = pool // 4
-            cut = min(pool + W2_SCALAR[e * 3 + q], w) // 8 * 2
-            src = w2_raw(e, q)[:].rearrange("p j (b i) -> p b j i", i=4)
-            dest = w2_bf(e, q)[:].rearrange("p (b i) j -> p b j i", i=4)
-            if cut > lo:
-                nc.scalar.activation(out=dest[:, lo:cut], in_=src[:, lo:cut], func=ACT.Copy)
-            if cut < w // 4:
-                nc.vector.tensor_copy(out=dest[:, cut:], in_=src[:, cut:])
-
-        def quant_w2(e, q):
-            n0, w = pieces[e][q]
-            for a, b in ((0, min(w, 256)), (256, w)):
-                if b > a:
-                    nc.vector.quantize_mx(
-                        out=w2_words(e)[:, n0 + a : n0 + b].bitcast(FP8X4),
-                        scales=w2_scales(e)[:, n0 + a : n0 + b],
-                        in_=w2_bf(e, q)[:, a:b, :].rearrange("p n j -> p (n j)"),
-                    )
-
-        def second_layer(e, c):
-            cols = slice(c * P, (c + 1) * P)
+        def second_layer(c, head_mx, rest_mx, dest):
+            words, scales = head_mx if c == 0 else rest_mx
+            cols = slice(0, P) if c == 0 else slice((c - 1) * P, c * P)
             nc.tensor.matmul_mx(
-                out=y_ps(e, c)[:],
-                lhsT=w2_words(e)[:, cols].bitcast(FP8X4),
-                lhsT_scale=w2_scales(e)[:, cols],
-                rhs=h_words(e)[:].bitcast(FP8X4),
-                rhs_scale=h_scales(e)[:],
+                out=dest,
+                lhsT=words[:, cols].bitcast(FP8X4),
+                lhsT_scale=scales[:, cols],
+                rhs=head_mx[0][:, P:].bitcast(FP8X4),
+                rhs_scale=head_mx[1][:, P:],
                 start=True,
                 stop=True,
             )
 
-        def gate_of(e):
-            return gate_sb(e * C // gw)[:, e * C % gw : e * C % gw + C]
+        y_sb = {}
 
-        def evacuate(e, c):
-            if GATEV[e][c] == "1":
-                nc.vector.tensor_tensor(out=y_sb(e, c)[:], in0=y_ps(e, c)[:], in1=gate_of(e), op=MULT)
-            else:
-                nc.scalar.activation(out=y_sb(e, c)[:], in_=y_ps(e, c)[:], func=ACT.Copy)
+        def leave_psum(e, sums, first, tag=None):
+            staged = sbuf(f"ysb{e}{first}", list(sums.shape), F32, tag)
+            nc.scalar.copy(out=staged[:], in_=sums)
+            for u in range(sums.shape[1]):
+                y_sb[e, first + u] = staged[:, u, :]
 
-        def scatter(e, c):
-            lst = dst_sb[:, e * LIST_COLS : (e + 1) * LIST_COLS]
-            if GATEV[e][c] == "1":
-                nc.vector.tensor_copy(out_sb[c][:].indirect(lst), y_sb(e, c)[:])
-            else:
-                nc.vector.tensor_tensor(out_sb[c][:].indirect(lst), y_sb(e, c)[:], gate_of(e), MULT)
-
-        def store(c):
-            nc.sync.dma_start(out=out[c * P : (c + 1) * P, :], in_=out_sb[c][:])
-
+        on_scalar, on_vector = nc.scalar.copy, nc.vector.tensor_copy
         spread_gate()
         gather(0)
+        y_bank = None
         for e in range(E):
+            banks = [psum.tile([P, C], F32, name=f"a{e}{t}", tag=f"a{t}") for t in range(PACK)]
             for o in range(PASSES):
-                round_w1(e, o)
-                quant_w1(e, o)
-                first_layer(e, o)
-            if e > 0 and not EVLATE:
-                for c in range(EARLY, CHUNKS - (e == E - 1 and LATE2)):
-                    evacuate(e - 1, c)
-            relu(e)
-            square(e)
-            quant_h(e)
-            if e == E - 1 and LATE2:
-                evacuate(e - 1, CHUNKS - 1)
-            for q in range(len(pieces[e])):
-                round_w2(e, q)
-                quant_w2(e, q)
-            if e > 0 and EVLATE:
+                first_layer_pass(e, o, banks)
+
+            if e > 0:
+                now = CHUNKS - 1 if e == LAST else CHUNKS
+                leave_psum(e - 1, y_bank[:, :now, :], 0, f"w1raw{e}{PASSES - 1}")
+
+            relu = sbuf(f"relu{e}", [P, PACK, C], F32)
+            for t in range(PACK):
+                nc.scalar.activation(out=relu[:, t, :], in_=banks[t][:], func=ACT.Relu)
+            head = sbuf(f"head{e}", [P, P + C, PACK], BF16)
+            rest = sbuf(f"rest{e}", [P, N - P, PACK], BF16, f"w1bf{e}{PASSES - 1}" if e == LAST else None)
+            nc.scalar.activation(out=head[:, P:, :], in_=relu[:].rearrange("p t s -> p s t"), func=ACT.Square)
+            head_mx = (sbuf(f"head_w{e}", [P, P + C], U32), sbuf(f"head_s{e}", [P, P + C], U8))
+            rest_mx = (sbuf(f"rest_w{e}", [P, N - P], U32), sbuf(f"rest_s{e}", [P, N - P], U8))
+
+            if e < LAST:
+                copy = on_vector if e == 0 else on_scalar
+                round_w2(copy, e, 0, head[:, :P, :])
+                round_w2(copy, e, P, rest[:])
+                quantise(head_mx, head, 0, P + C)
+                quantise(rest_mx, rest, 0, N - P)
+                y_bank = psum.tile([P, CHUNKS, C], F32, name=f"y{e}", tag=f"y{e % 2}")
                 for c in range(CHUNKS):
-                    evacuate(e - 1, c)
-            for c in range(CHUNKS):
-                second_layer(e, c)
-                if c < EARLY or e == E - 1:
-                    evacuate(e, c)
+                    second_layer(c, head_mx, rest_mx, y_bank[:, c, :])
+            else:
+                quantise(head_mx, head, P, P + C)
+                leave_psum(e - 1, y_bank[:, CHUNKS - 1 :, :], CHUNKS - 1, f"relu{e}")
+                round_w2(on_scalar, e, 0, head[:, :P, :])
+                quantise(head_mx, head, 0, P)
+                round_w2(on_scalar, e, P, rest[:, :LAST_CHUNK1_ON_SCALAR, :])
+                round_w2(on_vector, e, P + LAST_CHUNK1_ON_SCALAR, rest[:, LAST_CHUNK1_ON_SCALAR:P, :])
+                quantise(rest_mx, rest, 0, P)
+                round_w2(on_scalar, e, 2 * P, rest[:, P:, :])
+                quantise(rest_mx, rest, P, 2 * P)
+                for c, tag in enumerate(("y1", "y2", "a0")):
+                    bank = psum.tile([P, 1, C], F32, name=f"y{e}{c}", tag=tag)
+                    second_layer(c, head_mx, rest_mx, bank[:, 0, :])
+                    leave_psum(e, bank[:], c)
             if e == 0:
                 gather(1)
+
         for e in range(E):
+            entries = dst_sb[:, e * C // PER_COL : (e + 1) * C // PER_COL]
             for c in range(CHUNKS):
-                scatter(e, c)
+                nc.vector.tensor_tensor(out_sb[c][:].indirect(entries), y_sb[e, c], gate_sb[:, e * C : (e + 1) * C], MULT)
         for c in range(CHUNKS):
-            store(c)
+            nc.sync.dma_start(out=out[c * P : (c + 1) * P, :], in_=out_sb[c][:])

@@ -25,9 +25,7 @@ QUADRANT = 32
 HALF = SLOTS // 2
 LAST = E - 1
 
-W1_ON_SCALAR = (48, 72)
-LAST_PASS_ON_SCALAR = 80
-LAST_CHUNK1_ON_SCALAR = 32
+W1_ON_SCALAR = (P // 3, 5 * P // 8)
 
 FLOPS = 2 * SLOTS * (K * H + H * N)
 
@@ -108,14 +106,14 @@ def tile_moe_two_mlp_relu2_kernel(tc, x_words, x_scales, w1, w2, gate, offs, dst
             rounded = sbuf(f"w1bf{e}{o}", [P, PACK, P, PACK], BF16)
             src = w1_raw[e, o][:].rearrange("p j (m t) -> p m j t", t=PACK)
             dest = rounded[:].rearrange("p t m j -> p m j t")
-            cut = LAST_PASS_ON_SCALAR if (e, o) == (LAST, PASSES - 1) else W1_ON_SCALAR[o]
+            cut = W1_ON_SCALAR[o]
             nc.scalar.copy(out=dest[:, :cut], in_=src[:, :cut])
             nc.vector.tensor_copy(out=dest[:, cut:], in_=src[:, cut:])
 
             words = sbuf(f"w1w{e}{o}", [P, H], U32)
             scales = sbuf(f"w1s{e}{o}", [P, H], U8)
             flat = rounded[:].rearrange("p t m j -> p (t m j)")
-            step = P if o == PASSES - 1 else H
+            step = H if o < PASSES - 1 else P if e == LAST else H // 2
             for a in range(0, H, step):
                 nc.vector.quantize_mx(
                     out=words[:, a : a + step].bitcast(FP8X4),
@@ -205,8 +203,7 @@ def tile_moe_two_mlp_relu2_kernel(tc, x_words, x_scales, w1, w2, gate, offs, dst
                 leave_psum(e - 1, y_bank[:, CHUNKS - 1 :, :], CHUNKS - 1, f"relu{e}")
                 round_w2(on_scalar, e, 0, head[:, :P, :])
                 quantise(head_mx, head, 0, P)
-                round_w2(on_scalar, e, P, rest[:, :LAST_CHUNK1_ON_SCALAR, :])
-                round_w2(on_vector, e, P + LAST_CHUNK1_ON_SCALAR, rest[:, LAST_CHUNK1_ON_SCALAR:P, :])
+                round_w2(on_vector, e, P, rest[:, :P, :])
                 quantise(rest_mx, rest, 0, P)
                 round_w2(on_scalar, e, 2 * P, rest[:, P:, :])
                 quantise(rest_mx, rest, P, 2 * P)

@@ -25,7 +25,7 @@ QUADRANT = 32
 HALF = SLOTS // 2
 LAST = E - 1
 
-W1_ON_SCALAR = (P // 3, 5 * P // 8)
+W1_ON_SCALAR = (P // 3, P // 2)
 
 FLOPS = 2 * SLOTS * (K * H + H * N)
 
@@ -68,11 +68,11 @@ def tile_moe_two_mlp_relu2_kernel(tc, x_words, x_scales, w1, w2, gate, offs, dst
             w2_raw[e] = sbuf(f"w2raw{e}", [P, PACK, N], F32)
             nc.sync.dma_start(out=w2_raw[e][:], in_=w2[e].rearrange("(p j) n -> p j n", j=PACK))
 
-        nc.sync.dma_start(offs_sb[:], offs)
         nc.sync.dma_start(
             out=tok_words[:].rearrange("p (o t) -> p o t", o=PASSES),
             in_=x_words.rearrange("o p t r -> p o (t r)").bitcast(I32),
         )
+        nc.sync.dma_start(offs_sb[:], offs)
         load_w1(0, 0)
         for q in range(P // QUADRANT):
             nc.sync.dma_start(
@@ -108,7 +108,11 @@ def tile_moe_two_mlp_relu2_kernel(tc, x_words, x_scales, w1, w2, gate, offs, dst
             dest = rounded[:].rearrange("p t m j -> p m j t")
             cut = W1_ON_SCALAR[o]
             nc.scalar.copy(out=dest[:, :cut], in_=src[:, :cut])
-            nc.vector.tensor_copy(out=dest[:, cut:], in_=src[:, cut:])
+            if o < PASSES - 1:
+                nc.vector.tensor_copy(out=dest[:, cut:], in_=src[:, cut:])
+            else:
+                for t in range(0, PACK, 2):
+                    nc.vector.tensor_copy(out=dest[:, cut:, :, t : t + 2], in_=src[:, cut:, :, t : t + 2])
 
             words = sbuf(f"w1w{e}{o}", [P, H], U32)
             scales = sbuf(f"w1s{e}{o}", [P, H], U8)
@@ -146,24 +150,23 @@ def tile_moe_two_mlp_relu2_kernel(tc, x_words, x_scales, w1, w2, gate, offs, dst
                 in_=rounded[:, first:end, :].rearrange("p n j -> p (n j)"),
             )
 
-        def second_layer(c, head_mx, rest_mx, dest):
-            words, scales = head_mx if c == 0 else rest_mx
-            cols = slice(0, P) if c == 0 else slice((c - 1) * P, c * P)
+        def second_layer(mx, c, dest):
+            words, scales = mx
+            cols = slice(C + c * P, C + (c + 1) * P)
             nc.tensor.matmul_mx(
                 out=dest,
                 lhsT=words[:, cols].bitcast(FP8X4),
                 lhsT_scale=scales[:, cols],
-                rhs=head_mx[0][:, P:].bitcast(FP8X4),
-                rhs_scale=head_mx[1][:, P:],
+                rhs=words[:, :C].bitcast(FP8X4),
+                rhs_scale=scales[:, :C],
                 start=True,
                 stop=True,
             )
 
         y_sb = {}
 
-        def leave_psum(e, sums, first, tag=None):
-            staged = sbuf(f"ysb{e}{first}", list(sums.shape), F32, tag)
-            nc.scalar.copy(out=staged[:], in_=sums)
+        def leave_psum(e, sums, first, staged):
+            nc.scalar.copy(out=staged, in_=sums)
             for u in range(sums.shape[1]):
                 y_sb[e, first + u] = staged[:, u, :]
 
@@ -178,39 +181,44 @@ def tile_moe_two_mlp_relu2_kernel(tc, x_words, x_scales, w1, w2, gate, offs, dst
 
             if e > 0:
                 now = CHUNKS - 1 if e == LAST else CHUNKS
-                leave_psum(e - 1, y_bank[:, :now, :], 0, f"w1raw{e}{PASSES - 1}")
+                staged = sbuf(f"ysb{e - 1}", [P, now, C], F32, f"w1raw{e}{PASSES - 1}")
+                leave_psum(e - 1, y_bank[:, :now, :], 0, staged[:])
 
             relu = sbuf(f"relu{e}", [P, PACK, C], F32)
             for t in range(PACK):
                 nc.scalar.activation(out=relu[:, t, :], in_=banks[t][:], func=ACT.Relu)
-            head = sbuf(f"head{e}", [P, P + C, PACK], BF16)
-            rest = sbuf(f"rest{e}", [P, N - P, PACK], BF16, f"w1bf{e}{PASSES - 1}" if e == LAST else None)
-            nc.scalar.activation(out=head[:, P:, :], in_=relu[:].rearrange("p t s -> p s t"), func=ACT.Square)
-            head_mx = (sbuf(f"head_w{e}", [P, P + C], U32), sbuf(f"head_s{e}", [P, P + C], U8))
-            rest_mx = (sbuf(f"rest_w{e}", [P, N - P], U32), sbuf(f"rest_s{e}", [P, N - P], U8))
+            second = sbuf(f"second{e}", [P, C + N, PACK], BF16)
+            mx = (sbuf(f"second_w{e}", [P, C + N], U32), sbuf(f"second_s{e}", [P, C + N], U8))
+            nc.scalar.activation(
+                out=second[:, :C, :].rearrange("p (b u) t -> p b t u", u=4),
+                in_=relu[:].rearrange("p t (b u) -> p b t u", u=4),
+                func=ACT.Square,
+            )
 
             if e < LAST:
                 copy = on_vector if e == 0 else on_scalar
-                round_w2(copy, e, 0, head[:, :P, :])
-                round_w2(copy, e, P, rest[:])
-                quantise(head_mx, head, 0, P + C)
-                quantise(rest_mx, rest, 0, N - P)
+                round_w2(copy, e, 0, second[:, C : C + P, :])
+                round_w2(copy, e, P, second[:, C + P :, :])
+                quantise(mx, second, 0, C + N)
                 y_bank = psum.tile([P, CHUNKS, C], F32, name=f"y{e}", tag=f"y{e % 2}")
                 for c in range(CHUNKS):
-                    second_layer(c, head_mx, rest_mx, y_bank[:, c, :])
+                    second_layer(mx, c, y_bank[:, c, :])
             else:
-                quantise(head_mx, head, P, P + C)
-                leave_psum(e - 1, y_bank[:, CHUNKS - 1 :, :], CHUNKS - 1, f"relu{e}")
-                round_w2(on_scalar, e, 0, head[:, :P, :])
-                quantise(head_mx, head, 0, P)
-                round_w2(on_vector, e, P, rest[:, :P, :])
-                quantise(rest_mx, rest, 0, P)
-                round_w2(on_scalar, e, 2 * P, rest[:, P:, :])
-                quantise(rest_mx, rest, P, 2 * P)
+                round_w2(on_scalar, e, 0, second[:, C : C + P, :])
+                quantise(mx, second, 0, C + P)
+                leave_psum(e - 1, y_bank[:, CHUNKS - 1 :, :], CHUNKS - 1, relu[:, 0:1, :])
+                middle = sbuf("middle", [P, P, PACK], BF16, f"w1bf{e}{PASSES - 1}")
+                late = relu[:, 2:4, :].rearrange("p t s -> p (t s)").bitcast(BF16).rearrange("p (n j) -> p n j", j=PACK)
+                for c, copy, rounded in ((1, on_vector, middle[:]), (2, on_scalar, late)):
+                    cols = slice(C + c * P, C + (c + 1) * P)
+                    round_w2(copy, e, c * P, rounded)
+                    nc.vector.quantize_mx(
+                        out=mx[0][:, cols].bitcast(FP8X4), scales=mx[1][:, cols], in_=rounded.rearrange("p n j -> p (n j)")
+                    )
                 for c, tag in enumerate(("y1", "y2", "a0")):
                     bank = psum.tile([P, 1, C], F32, name=f"y{e}{c}", tag=tag)
-                    second_layer(c, head_mx, rest_mx, bank[:, 0, :])
-                    leave_psum(e, bank[:], c)
+                    second_layer(mx, c, bank[:, 0, :])
+                    leave_psum(e, bank[:], c, sbuf(f"ysb{e}{c}", [P, 1, C], F32)[:])
             if e == 0:
                 gather(1)
 

@@ -25,7 +25,6 @@ QUADRANT = 32
 HALF = SLOTS // 2
 LAST = E - 1
 
-W1_ON_SCALAR = (P // 3, P // 2)
 
 FLOPS = 2 * SLOTS * (K * H + H * N)
 
@@ -106,7 +105,7 @@ def tile_moe_two_mlp_relu2_kernel(tc, x_words, x_scales, w1, w2, gate, offs, dst
             rounded = sbuf(f"w1bf{e}{o}", [P, PACK, P, PACK], BF16)
             src = w1_raw[e, o][:].rearrange("p j (m t) -> p m j t", t=PACK)
             dest = rounded[:].rearrange("p t m j -> p m j t")
-            cut = W1_ON_SCALAR[o]
+            cut = 3 * P // 8 if o == 0 else 9 * P // 16
             nc.scalar.copy(out=dest[:, :cut], in_=src[:, :cut])
             if o < PASSES - 1:
                 nc.vector.tensor_copy(out=dest[:, cut:], in_=src[:, cut:])
@@ -204,17 +203,18 @@ def tile_moe_two_mlp_relu2_kernel(tc, x_words, x_scales, w1, w2, gate, offs, dst
                 for c in range(CHUNKS):
                     second_layer(mx, c, y_bank[:, c, :])
             else:
-                round_w2(on_scalar, e, 0, second[:, C : C + P, :])
-                quantise(mx, second, 0, C + P)
+                quantise(mx, second, 0, C)
                 leave_psum(e - 1, y_bank[:, CHUNKS - 1 :, :], CHUNKS - 1, relu[:, 0:1, :])
-                middle = sbuf("middle", [P, P, PACK], BF16, f"w1bf{e}{PASSES - 1}")
+                round_w2(on_scalar, e, 0, second[:, C : C + P, :])
+                round_w2(on_vector, e, P, second[:, C + P : C + 2 * P, :])
+                quantise(mx, second, C, C + 2 * P)
                 late = relu[:, 2:4, :].rearrange("p t s -> p (t s)").bitcast(BF16).rearrange("p (n j) -> p n j", j=PACK)
-                for c, copy, rounded in ((1, on_vector, middle[:]), (2, on_scalar, late)):
-                    cols = slice(C + c * P, C + (c + 1) * P)
-                    round_w2(copy, e, c * P, rounded)
-                    nc.vector.quantize_mx(
-                        out=mx[0][:, cols].bitcast(FP8X4), scales=mx[1][:, cols], in_=rounded.rearrange("p n j -> p (n j)")
-                    )
+                round_w2(on_scalar, e, 2 * P, late)
+                nc.vector.quantize_mx(
+                    out=mx[0][:, C + 2 * P :].bitcast(FP8X4),
+                    scales=mx[1][:, C + 2 * P :],
+                    in_=late.rearrange("p n j -> p (n j)"),
+                )
                 for c, tag in enumerate(("y1", "y2", "a0")):
                     bank = psum.tile([P, 1, C], F32, name=f"y{e}{c}", tag=tag)
                     second_layer(mx, c, bank[:, 0, :])

@@ -180,19 +180,20 @@ def tile_moe_two_mlp_relu2_kernel(tc, x_words, x_scales, w1, w2, gate, offs, dst
 
             if e > 0:
                 now = CHUNKS - 1 if e == LAST else CHUNKS
-                staged = sbuf(f"ysb{e - 1}", [P, now, C], F32, f"w1raw{e}{PASSES - 1}")
-                leave_psum(e - 1, y_bank[:, :now, :], 0, staged[:])
+                leave_psum(e - 1, y_bank[:, :now, :], 0, w1_raw[e, PASSES - 1][:, :now, :C])
 
             relu = sbuf(f"relu{e}", [P, PACK, C], F32)
             for t in range(PACK):
                 nc.scalar.activation(out=relu[:, t, :], in_=banks[t][:], func=ACT.Relu)
             second = sbuf(f"second{e}", [P, C + N, PACK], BF16)
             mx = (sbuf(f"second_w{e}", [P, C + N], U32), sbuf(f"second_s{e}", [P, C + N], U8))
-            nc.scalar.activation(
-                out=second[:, :C, :].rearrange("p (b u) t -> p b t u", u=4),
-                in_=relu[:].rearrange("p t (b u) -> p b t u", u=4),
-                func=ACT.Square,
-            )
+            width = PACK // 2 if e == LAST else PACK
+            for t in range(0, PACK, width):
+                nc.scalar.activation(
+                    out=second[:, :C, t : t + width].rearrange("p (b u) t -> p b t u", u=4),
+                    in_=relu[:, t : t + width, :].rearrange("p t (b u) -> p b t u", u=4),
+                    func=ACT.Square,
+                )
 
             if e < LAST:
                 copy = on_vector if e == 0 else on_scalar
@@ -203,12 +204,12 @@ def tile_moe_two_mlp_relu2_kernel(tc, x_words, x_scales, w1, w2, gate, offs, dst
                 for c in range(CHUNKS):
                     second_layer(mx, c, y_bank[:, c, :])
             else:
-                quantise(mx, second, 0, C)
-                leave_psum(e - 1, y_bank[:, CHUNKS - 1 :, :], CHUNKS - 1, relu[:, 0:1, :])
                 round_w2(on_scalar, e, 0, second[:, C : C + P, :])
+                quantise(mx, second, 0, C + P)
+                leave_psum(e - 1, y_bank[:, CHUNKS - 1 :, :], CHUNKS - 1, relu[:, 2:3, :])
                 round_w2(on_vector, e, P, second[:, C + P : C + 2 * P, :])
-                quantise(mx, second, C, C + 2 * P)
-                late = relu[:, 2:4, :].rearrange("p t s -> p (t s)").bitcast(BF16).rearrange("p (n j) -> p n j", j=PACK)
+                quantise(mx, second, C + P, C + 2 * P)
+                late = relu[:, 0:2, :].rearrange("p t s -> p (t s)").bitcast(BF16).rearrange("p (n j) -> p n j", j=PACK)
                 round_w2(on_scalar, e, 2 * P, late)
                 nc.vector.quantize_mx(
                     out=mx[0][:, C + 2 * P :].bitcast(FP8X4),

@@ -25,6 +25,10 @@ QUADRANT = 32
 HALF = SLOTS // 2
 LAST = E - 1
 
+SCALE_ROWS = 4
+RUN = 4
+
+W1_ON_SCALAR = (7 * P // 16, 9 * P // 16)
 
 FLOPS = 2 * SLOTS * (K * H + H * N)
 
@@ -75,8 +79,8 @@ def tile_moe_two_mlp_relu2_kernel(tc, x_words, x_scales, w1, w2, gate, offs, dst
         load_w1(0, 0)
         for q in range(P // QUADRANT):
             nc.sync.dma_start(
-                out=tok_scales[QUADRANT * q : QUADRANT * q + 4 * PASSES, :].bitcast(I32),
-                in_=x_scales[:, 4 * q : 4 * q + 4, :].bitcast(I32),
+                out=tok_scales[QUADRANT * q : QUADRANT * q + SCALE_ROWS * PASSES, :].bitcast(I32),
+                in_=x_scales[:, SCALE_ROWS * q : SCALE_ROWS * (q + 1), :].bitcast(I32),
             )
         nc.sync.dma_start(out=gate_row[:], in_=gate[0, :].rearrange("(p j) -> p j", j=PACK))
         load_w1(0, 1)
@@ -105,13 +109,14 @@ def tile_moe_two_mlp_relu2_kernel(tc, x_words, x_scales, w1, w2, gate, offs, dst
             rounded = sbuf(f"w1bf{e}{o}", [P, PACK, P, PACK], BF16)
             src = w1_raw[e, o][:].rearrange("p j (m t) -> p m j t", t=PACK)
             dest = rounded[:].rearrange("p t m j -> p m j t")
-            cut = 3 * P // 8 if o == 0 else 9 * P // 16
+            cut = W1_ON_SCALAR[o]
             nc.scalar.copy(out=dest[:, :cut], in_=src[:, :cut])
             if o < PASSES - 1:
                 nc.vector.tensor_copy(out=dest[:, cut:], in_=src[:, cut:])
             else:
-                for t in range(0, PACK, 2):
-                    nc.vector.tensor_copy(out=dest[:, cut:, :, t : t + 2], in_=src[:, cut:, :, t : t + 2])
+                for t in range(0, PACK, PACK // 2):
+                    half = slice(t, t + PACK // 2)
+                    nc.vector.tensor_copy(out=dest[:, cut:, :, half], in_=src[:, cut:, :, half])
 
             words = sbuf(f"w1w{e}{o}", [P, H], U32)
             scales = sbuf(f"w1s{e}{o}", [P, H], U8)
@@ -132,21 +137,22 @@ def tile_moe_two_mlp_relu2_kernel(tc, x_words, x_scales, w1, w2, gate, offs, dst
                     lhsT=words[:, cols].bitcast(FP8X4),
                     lhsT_scale=scales[:, cols],
                     rhs=slot_words[o][:, slots].bitcast(FP8X4),
-                    rhs_scale=slot_scales[4 * o :, slots],
+                    rhs_scale=slot_scales[SCALE_ROWS * o :, slots],
                     start=(o == 0),
                     stop=(o == PASSES - 1),
                 )
 
         def round_w2(copy, e, first, dest):
             src = w2_raw[e][:, :, first : first + dest.shape[1]]
-            copy(out=dest.rearrange("p (b u) j -> p b j u", u=4), in_=src.rearrange("p j (b u) -> p b j u", u=4))
+            copy(out=dest.rearrange("p (b u) j -> p b j u", u=RUN), in_=src.rearrange("p j (b u) -> p b j u", u=RUN))
 
-        def quantise(mx, rounded, first, end):
+        def quantise(mx, first, rounded):
             words, scales = mx
+            cols = slice(first, first + rounded.shape[1])
             nc.vector.quantize_mx(
-                out=words[:, first:end].bitcast(FP8X4),
-                scales=scales[:, first:end],
-                in_=rounded[:, first:end, :].rearrange("p n j -> p (n j)"),
+                out=words[:, cols].bitcast(FP8X4),
+                scales=scales[:, cols],
+                in_=rounded.rearrange("p n j -> p (n j)"),
             )
 
         def second_layer(mx, c, dest):
@@ -187,11 +193,11 @@ def tile_moe_two_mlp_relu2_kernel(tc, x_words, x_scales, w1, w2, gate, offs, dst
                 nc.scalar.activation(out=relu[:, t, :], in_=banks[t][:], func=ACT.Relu)
             second = sbuf(f"second{e}", [P, C + N, PACK], BF16)
             mx = (sbuf(f"second_w{e}", [P, C + N], U32), sbuf(f"second_s{e}", [P, C + N], U8))
-            width = PACK // 2 if e == LAST else PACK
-            for t in range(0, PACK, width):
+            planes = PACK // 2 if e == LAST else PACK
+            for t in range(0, PACK, planes):
                 nc.scalar.activation(
-                    out=second[:, :C, t : t + width].rearrange("p (b u) t -> p b t u", u=4),
-                    in_=relu[:, t : t + width, :].rearrange("p t (b u) -> p b t u", u=4),
+                    out=second[:, :C, t : t + planes].rearrange("p (b u) t -> p b t u", u=RUN),
+                    in_=relu[:, t : t + planes, :].rearrange("p t (b u) -> p b t u", u=RUN),
                     func=ACT.Square,
                 )
 
@@ -199,23 +205,19 @@ def tile_moe_two_mlp_relu2_kernel(tc, x_words, x_scales, w1, w2, gate, offs, dst
                 copy = on_vector if e == 0 else on_scalar
                 round_w2(copy, e, 0, second[:, C : C + P, :])
                 round_w2(copy, e, P, second[:, C + P :, :])
-                quantise(mx, second, 0, C + N)
+                quantise(mx, 0, second[:])
                 y_bank = psum.tile([P, CHUNKS, C], F32, name=f"y{e}", tag=f"y{e % 2}")
                 for c in range(CHUNKS):
                     second_layer(mx, c, y_bank[:, c, :])
             else:
                 round_w2(on_scalar, e, 0, second[:, C : C + P, :])
-                quantise(mx, second, 0, C + P)
+                quantise(mx, 0, second[:, : C + P, :])
                 leave_psum(e - 1, y_bank[:, CHUNKS - 1 :, :], CHUNKS - 1, relu[:, 2:3, :])
                 round_w2(on_vector, e, P, second[:, C + P : C + 2 * P, :])
-                quantise(mx, second, C + P, C + 2 * P)
+                quantise(mx, C + P, second[:, C + P : C + 2 * P, :])
                 late = relu[:, 0:2, :].rearrange("p t s -> p (t s)").bitcast(BF16).rearrange("p (n j) -> p n j", j=PACK)
                 round_w2(on_scalar, e, 2 * P, late)
-                nc.vector.quantize_mx(
-                    out=mx[0][:, C + 2 * P :].bitcast(FP8X4),
-                    scales=mx[1][:, C + 2 * P :],
-                    in_=late.rearrange("p n j -> p (n j)"),
-                )
+                quantise(mx, C + 2 * P, late)
                 for c, tag in enumerate(("y1", "y2", "a0")):
                     bank = psum.tile([P, 1, C], F32, name=f"y{e}{c}", tag=tag)
                     second_layer(mx, c, bank[:, 0, :])

@@ -28,7 +28,7 @@ LAST = E - 1
 SCALE_ROWS = 4
 RUN = 4
 
-W1_ON_SCALAR = (7 * P // 16, 9 * P // 16)
+W1_ON_SCALAR = (5 * P // 16, 9 * P // 16)
 
 FLOPS = 2 * SLOTS * (K * H + H * N)
 

@@ -28,7 +28,8 @@ LAST = E - 1
 SCALE_ROWS = 4
 RUN = 4
 
-W1_ON_SCALAR = (5 * P // 16, 9 * P // 16)
+HEAD_ON_SCALAR = (3 * P // 4, 3 * P // 8)
+PASS0_ON_SCALAR = 3 * P // 8
 
 FLOPS = 2 * SLOTS * (K * H + H * N)
 
@@ -92,7 +93,7 @@ def tile_moe_two_mlp_relu2_kernel(tc, x_words, x_scales, w1, w2, gate, offs, dst
             load_w2(e)
 
         def spread_gate():
-            spread = psum.tile([P, PACK, P], F32, name="gate_ps")
+            spread = psum.tile([P, PACK, P], F32, name="gate_ps", tag="y0")
             for j in range(PACK):
                 nc.tensor.transpose(spread[:, j, :], gate_row[:, j : j + 1].to_broadcast([P, P]), ident[:])
             nc.scalar.copy(out=gate_sb[:].rearrange("p (s j) -> p s j", j=PACK), in_=spread[:].rearrange("p j s -> p s j"))
@@ -105,23 +106,23 @@ def tile_moe_two_mlp_relu2_kernel(tc, x_words, x_scales, w1, w2, gate, offs, dst
                 nc.vector.tensor_copy(slot_words[o][:, cols], window.indirect(entries))
             nc.vector.tensor_copy(slot_scales[:, cols], tok_scales[:].indirect(entries))
 
-        def first_layer_pass(e, o, banks):
-            rounded = sbuf(f"w1bf{e}{o}", [P, PACK, P, PACK], BF16)
+        w1_bf = {}
+
+        def round_w1(e, o, cut, pieces):
+            rounded = w1_bf[e, o] = sbuf(f"w1bf{e}{o}", [P, PACK, P, PACK], BF16)
             src = w1_raw[e, o][:].rearrange("p j (m t) -> p m j t", t=PACK)
             dest = rounded[:].rearrange("p t m j -> p m j t")
-            cut = W1_ON_SCALAR[o]
-            nc.scalar.copy(out=dest[:, :cut], in_=src[:, :cut])
-            if o < PASSES - 1:
-                nc.vector.tensor_copy(out=dest[:, cut:], in_=src[:, cut:])
-            else:
-                for t in range(0, PACK, PACK // 2):
-                    half = slice(t, t + PACK // 2)
-                    nc.vector.tensor_copy(out=dest[:, cut:, :, half], in_=src[:, cut:, :, half])
+            if cut > 0:
+                nc.scalar.copy(out=dest[:, :cut], in_=src[:, :cut])
+            for t in range(0, PACK, PACK // pieces):
+                part = slice(t, t + PACK // pieces)
+                nc.vector.tensor_copy(out=dest[:, cut:, :, part], in_=src[:, cut:, :, part])
 
+        def first_layer_pass(e, o, banks, pieces):
             words = sbuf(f"w1w{e}{o}", [P, H], U32)
             scales = sbuf(f"w1s{e}{o}", [P, H], U8)
-            flat = rounded[:].rearrange("p t m j -> p (t m j)")
-            step = H if o < PASSES - 1 else P if e == LAST else H // 2
+            flat = w1_bf[e, o][:].rearrange("p t m j -> p (t m j)")
+            step = H // pieces
             for a in range(0, H, step):
                 nc.vector.quantize_mx(
                     out=words[:, a : a + step].bitcast(FP8X4),
@@ -168,66 +169,76 @@ def tile_moe_two_mlp_relu2_kernel(tc, x_words, x_scales, w1, w2, gate, offs, dst
                 stop=True,
             )
 
-        y_sb = {}
+        def times_gate(e, sums, dest):
+            weights = gate_sb[:, e * C : (e + 1) * C].unsqueeze(1).to_broadcast(list(sums.shape))
+            nc.vector.tensor_tensor(dest, sums, weights, MULT)
 
-        def leave_psum(e, sums, first, staged):
-            nc.scalar.copy(out=staged, in_=sums)
-            for u in range(sums.shape[1]):
-                y_sb[e, first + u] = staged[:, u, :]
+        rounded2 = [sbuf(f"second{e}", [P, C + N, PACK], BF16) for e in range(E)]
+        mx2 = [(sbuf(f"second_w{e}", [P, C + N], U32), sbuf(f"second_s{e}", [P, C + N], U8)) for e in range(E)]
 
-        on_scalar, on_vector = nc.scalar.copy, nc.vector.tensor_copy
-        spread_gate()
-        gather(0)
-        y_bank = None
-        for e in range(E):
-            banks = [psum.tile([P, C], F32, name=f"a{e}{t}", tag=f"a{t}") for t in range(PACK)]
-            for o in range(PASSES):
-                first_layer_pass(e, o, banks)
-
-            if e > 0:
-                now = CHUNKS - 1 if e == LAST else CHUNKS
-                leave_psum(e - 1, y_bank[:, :now, :], 0, w1_raw[e, PASSES - 1][:, :now, :C])
-
+        def relu_squared(e, banks):
             relu = sbuf(f"relu{e}", [P, PACK, C], F32)
-            for t in range(PACK):
-                nc.scalar.activation(out=relu[:, t, :], in_=banks[t][:], func=ACT.Relu)
-            second = sbuf(f"second{e}", [P, C + N, PACK], BF16)
-            mx = (sbuf(f"second_w{e}", [P, C + N], U32), sbuf(f"second_s{e}", [P, C + N], U8))
-            planes = PACK // 2 if e == LAST else PACK
-            for t in range(0, PACK, planes):
+            for t0 in range(0, PACK, 2):
+                for t in (t0, t0 + 1):
+                    nc.scalar.activation(out=relu[:, t, :], in_=banks[t][:], func=ACT.Relu)
                 nc.scalar.activation(
-                    out=second[:, :C, t : t + planes].rearrange("p (b u) t -> p b t u", u=RUN),
-                    in_=relu[:, t : t + planes, :].rearrange("p t (b u) -> p b t u", u=RUN),
+                    out=rounded2[e][:, :C, t0 : t0 + 2].rearrange("p (b u) t -> p b t u", u=RUN),
+                    in_=relu[:, t0 : t0 + 2, :].rearrange("p t (b u) -> p b t u", u=RUN),
                     func=ACT.Square,
                 )
 
-            if e < LAST:
-                copy = on_vector if e == 0 else on_scalar
-                round_w2(copy, e, 0, second[:, C : C + P, :])
-                round_w2(copy, e, P, second[:, C + P :, :])
-                quantise(mx, 0, second[:])
-                y_bank = psum.tile([P, CHUNKS, C], F32, name=f"y{e}", tag=f"y{e % 2}")
-                for c in range(CHUNKS):
-                    second_layer(mx, c, y_bank[:, c, :])
-            else:
-                round_w2(on_scalar, e, 0, second[:, C : C + P, :])
-                quantise(mx, 0, second[:, : C + P, :])
-                leave_psum(e - 1, y_bank[:, CHUNKS - 1 :, :], CHUNKS - 1, relu[:, 2:3, :])
-                round_w2(on_vector, e, P, second[:, C + P : C + 2 * P, :])
-                quantise(mx, C + P, second[:, C + P : C + 2 * P, :])
-                late = relu[:, 0:2, :].rearrange("p t s -> p (t s)").bitcast(BF16).rearrange("p (n j) -> p n j", j=PACK)
-                round_w2(on_scalar, e, 2 * P, late)
-                quantise(mx, C + 2 * P, late)
-                for c, tag in enumerate(("y1", "y2", "a0")):
-                    bank = psum.tile([P, 1, C], F32, name=f"y{e}{c}", tag=tag)
-                    second_layer(mx, c, bank[:, 0, :])
-                    leave_psum(e, bank[:], c, sbuf(f"ysb{e}{c}", [P, 1, C], F32)[:])
-            if e == 0:
-                gather(1)
+        def quantise_h(e):
+            quantise(mx2[e], 0, rounded2[e][:, :C, :])
 
+        def round_chunks(e, a, b):
+            round_w2(nc.vector.tensor_copy, e, a * P, rounded2[e][:, C + a * P : C + b * P, :])
+
+        def quantise_chunks(e, a, b):
+            quantise(mx2[e], C + a * P, rounded2[e][:, C + a * P : C + b * P, :])
+
+        def products(e, a, b, tag):
+            bank = psum.tile([P, b - a, C], F32, name=f"y{e}{a}", tag=tag)
+            for c in range(a, b):
+                second_layer(mx2[e], c, bank[:, c - a, :])
+            return bank
+
+        def scatter(e, c, values, on_vector):
+            window = out_sb[c][:].indirect(dst_sb[:, e * C // PER_COL : (e + 1) * C // PER_COL])
+            if on_vector:
+                nc.vector.tensor_copy(window, values)
+            else:
+                nc.scalar.activation(out=window, in_=values, func=ACT.Copy)
+
+        spread_gate()
+        gather(0)
+        gather(1)
+        y_bank = None
         for e in range(E):
-            entries = dst_sb[:, e * C // PER_COL : (e + 1) * C // PER_COL]
-            for c in range(CHUNKS):
-                nc.vector.tensor_tensor(out_sb[c][:].indirect(entries), y_sb[e, c], gate_sb[:, e * C : (e + 1) * C], MULT)
+            banks = [psum.tile([P, C], F32, name=f"a{e}{t}", tag=f"a{t}") for t in range(PACK)]
+            round_w1(e, 0, HEAD_ON_SCALAR[0] if e == 0 else PASS0_ON_SCALAR, 1)
+            if e > 0:
+                staged = w1_raw[e, 0][:, :CHUNKS, :C]
+                times_gate(e - 1, y_bank[:], staged)
+                for c in range(CHUNKS):
+                    scatter(e - 1, c, staged[:, c, :], False)
+            first_layer_pass(e, 0, banks, 1)
+            round_w1(e, 1, HEAD_ON_SCALAR[1] if e == 0 else 0, 2)
+            first_layer_pass(e, 1, banks, PACK if e == LAST else 2)
+            relu_squared(e, banks)
+            if e < LAST:
+                round_chunks(e, 0, CHUNKS)
+                quantise_chunks(e, 0, CHUNKS)
+                quantise_h(e)
+                y_bank = products(e, 0, CHUNKS, "y1")
+        round_chunks(LAST, 0, 1)
+        round_chunks(LAST, 1, CHUNKS)
+        quantise_chunks(LAST, 0, 1)
+        quantise_chunks(LAST, 1, CHUNKS)
+        quantise_h(LAST)
+        gated = sbuf("gated", [P, CHUNKS, C], F32)
+        times_gate(LAST, products(LAST, 0, 1, "y0")[:], gated[:, :1, :])
+        times_gate(LAST, products(LAST, 1, CHUNKS, "y2")[:], gated[:, 1:, :])
+        for c in range(CHUNKS):
+            scatter(LAST, c, gated[:, c, :], c == 1)
         for c in range(CHUNKS):
             nc.sync.dma_start(out=out[c * P : (c + 1) * P, :], in_=out_sb[c][:])

@@ -28,8 +28,9 @@ LAST = E - 1
 SCALE_ROWS = 4
 RUN = 4
 
-HEAD_ON_SCALAR = (3 * P // 4, 3 * P // 8)
+HEAD_ON_SCALAR = 3 * P // 4
 PASS0_ON_SCALAR = 3 * P // 8
+PASS1_ON_SCALAR = 3 * P // 8
 
 FLOPS = 2 * SLOTS * (K * H + H * N)
 
@@ -90,7 +91,10 @@ def tile_moe_two_mlp_relu2_kernel(tc, x_words, x_scales, w1, w2, gate, offs, dst
         for e in range(1, E):
             load_w1(e, 0)
             load_w1(e, 1)
-            load_w2(e)
+            if e < LAST - 1:
+                load_w2(e)
+        load_w2(LAST - 1)
+        load_w2(LAST)
 
         def spread_gate():
             spread = psum.tile([P, PACK, P], F32, name="gate_ps", tag="y0")
@@ -106,101 +110,76 @@ def tile_moe_two_mlp_relu2_kernel(tc, x_words, x_scales, w1, w2, gate, offs, dst
                 nc.vector.tensor_copy(slot_words[o][:, cols], window.indirect(entries))
             nc.vector.tensor_copy(slot_scales[:, cols], tok_scales[:].indirect(entries))
 
-        w1_bf = {}
-
-        def round_w1(e, o, cut, pieces):
-            rounded = w1_bf[e, o] = sbuf(f"w1bf{e}{o}", [P, PACK, P, PACK], BF16)
-            src = w1_raw[e, o][:].rearrange("p j (m t) -> p m j t", t=PACK)
-            dest = rounded[:].rearrange("p t m j -> p m j t")
-            if cut > 0:
-                nc.scalar.copy(out=dest[:, :cut], in_=src[:, :cut])
-            for t in range(0, PACK, PACK // pieces):
-                part = slice(t, t + PACK // pieces)
-                nc.vector.tensor_copy(out=dest[:, cut:, :, part], in_=src[:, cut:, :, part])
-
-        def first_layer_pass(e, o, banks, pieces):
-            words = sbuf(f"w1w{e}{o}", [P, H], U32)
-            scales = sbuf(f"w1s{e}{o}", [P, H], U8)
-            flat = w1_bf[e, o][:].rearrange("p t m j -> p (t m j)")
-            step = H // pieces
-            for a in range(0, H, step):
-                nc.vector.quantize_mx(
-                    out=words[:, a : a + step].bitcast(FP8X4),
-                    scales=scales[:, a : a + step],
-                    in_=flat[:, a * PACK : (a + step) * PACK],
-                )
-
-            slots = slice(e * C, (e + 1) * C)
-            for t in range(PACK):
-                cols = slice(t * P, (t + 1) * P)
-                nc.tensor.matmul_mx(
-                    out=banks[t][:],
-                    lhsT=words[:, cols].bitcast(FP8X4),
-                    lhsT_scale=scales[:, cols],
-                    rhs=slot_words[o][:, slots].bitcast(FP8X4),
-                    rhs_scale=slot_scales[SCALE_ROWS * o :, slots],
-                    start=(o == 0),
-                    stop=(o == PASSES - 1),
-                )
-
-        def round_w2(copy, e, first, dest):
-            src = w2_raw[e][:, :, first : first + dest.shape[1]]
-            copy(out=dest.rearrange("p (b u) j -> p b j u", u=RUN), in_=src.rearrange("p j (b u) -> p b j u", u=RUN))
-
-        def quantise(mx, first, rounded):
-            words, scales = mx
-            cols = slice(first, first + rounded.shape[1])
-            nc.vector.quantize_mx(
-                out=words[:, cols].bitcast(FP8X4),
-                scales=scales[:, cols],
-                in_=rounded.rearrange("p n j -> p (n j)"),
+        def operand(name, columns):
+            return (
+                sbuf(f"{name}_bf", [P, columns, PACK], BF16),
+                sbuf(f"{name}_w", [P, columns], U32),
+                sbuf(f"{name}_s", [P, columns], U8),
             )
 
-        def second_layer(mx, c, dest):
-            words, scales = mx
-            cols = slice(C + c * P, C + (c + 1) * P)
+        def quantise(op, first, last):
+            rounded, words, scales = op
+            nc.vector.quantize_mx(
+                out=words[:, first:last].bitcast(FP8X4),
+                scales=scales[:, first:last],
+                in_=rounded[:, first:last, :].rearrange("p n j -> p (n j)"),
+            )
+
+        def codes(op, first):
+            return op[1][:, first : first + P].bitcast(FP8X4), op[2][:, first : first + P]
+
+        def product(dest, stationary, moving, start, stop):
             nc.tensor.matmul_mx(
                 out=dest,
-                lhsT=words[:, cols].bitcast(FP8X4),
-                lhsT_scale=scales[:, cols],
-                rhs=words[:, :C].bitcast(FP8X4),
-                rhs_scale=scales[:, :C],
-                start=True,
-                stop=True,
+                lhsT=stationary[0],
+                lhsT_scale=stationary[1],
+                rhs=moving[0],
+                rhs_scale=moving[1],
+                start=start,
+                stop=stop,
             )
 
-        def times_gate(e, sums, dest):
-            weights = gate_sb[:, e * C : (e + 1) * C].unsqueeze(1).to_broadcast(list(sums.shape))
-            nc.vector.tensor_tensor(dest, sums, weights, MULT)
+        w1_op = {(e, o): operand(f"w1_{e}{o}", H) for e in range(E) for o in range(PASSES)}
+        w2_op = [operand(f"w2_{e}", N) for e in range(E)]
+        h_op = [(operand(f"h_{e}", C), 0) for e in range(E)]
 
-        rounded2 = [sbuf(f"second{e}", [P, C + N, PACK], BF16) for e in range(E)]
-        mx2 = [(sbuf(f"second_w{e}", [P, C + N], U32), sbuf(f"second_s{e}", [P, C + N], U8)) for e in range(E)]
+        def round_w1(copy, e, o, ms, ts):
+            src = w1_raw[e, o][:].rearrange("p j (m t) -> p m j t", t=PACK)
+            dest = w1_op[e, o][0][:, :H, :].rearrange("p (t m) j -> p m j t", t=PACK)
+            copy(out=dest[:, ms, :, ts], in_=src[:, ms, :, ts])
+
+        def first_layer(e, o, banks, ts):
+            slots = slice(e * C, (e + 1) * C)
+            tokens = slot_words[o][:, slots].bitcast(FP8X4), slot_scales[SCALE_ROWS * o :, slots]
+            for t in ts:
+                product(banks[t][:], codes(w1_op[e, o], t * P), tokens, o == 0, o == PASSES - 1)
+
+        def round_w2(copy, e, a, b):
+            src = w2_raw[e][:, :, a * P : b * P].rearrange("p j (g u) -> p g j u", u=RUN)
+            copy(out=w2_op[e][0][:, a * P : b * P, :].rearrange("p (g u) j -> p g j u", u=RUN), in_=src)
 
         def relu_squared(e, banks):
             relu = sbuf(f"relu{e}", [P, PACK, C], F32)
+            op, first = h_op[e]
             for t0 in range(0, PACK, 2):
                 for t in (t0, t0 + 1):
                     nc.scalar.activation(out=relu[:, t, :], in_=banks[t][:], func=ACT.Relu)
                 nc.scalar.activation(
-                    out=rounded2[e][:, :C, t0 : t0 + 2].rearrange("p (b u) t -> p b t u", u=RUN),
-                    in_=relu[:, t0 : t0 + 2, :].rearrange("p t (b u) -> p b t u", u=RUN),
+                    out=op[0][:, first : first + C, t0 : t0 + 2].rearrange("p (g u) t -> p g t u", u=RUN),
+                    in_=relu[:, t0 : t0 + 2, :].rearrange("p t (g u) -> p g t u", u=RUN),
                     func=ACT.Square,
                 )
+            return relu
 
-        def quantise_h(e):
-            quantise(mx2[e], 0, rounded2[e][:, :C, :])
-
-        def round_chunks(e, a, b):
-            round_w2(nc.vector.tensor_copy, e, a * P, rounded2[e][:, C + a * P : C + b * P, :])
-
-        def quantise_chunks(e, a, b):
-            quantise(mx2[e], C + a * P, rounded2[e][:, C + a * P : C + b * P, :])
-
-        def products(e, a, b, tag):
+        def second_layer(e, a, b, tag):
             bank = psum.tile([P, b - a, C], F32, name=f"y{e}{a}", tag=tag)
             for c in range(a, b):
-                second_layer(mx2[e], c, bank[:, c - a, :])
+                product(bank[:, c - a, :], codes(w2_op[e], c * P), codes(*h_op[e]), True, True)
             return bank
+
+        def times_gate(e, sums, dest):
+            weights = gate_sb[:, e * C : (e + 1) * C].unsqueeze(1).to_broadcast(list(sums.shape))
+            nc.vector.tensor_tensor(dest, sums, weights, MULT)
 
         def scatter(e, c, values, on_vector):
             window = out_sb[c][:].indirect(dst_sb[:, e * C // PER_COL : (e + 1) * C // PER_COL])
@@ -209,36 +188,78 @@ def tile_moe_two_mlp_relu2_kernel(tc, x_words, x_scales, w1, w2, gate, offs, dst
             else:
                 nc.scalar.activation(out=window, in_=values, func=ACT.Copy)
 
+        on_scalar, on_vector = nc.scalar.copy, nc.vector.tensor_copy
+        low, high, both = slice(0, PACK // 2), slice(PACK // 2, PACK), slice(0, PACK)
         spread_gate()
         gather(0)
         gather(1)
-        y_bank = None
+        y_first = y_rest = None
         for e in range(E):
             banks = [psum.tile([P, C], F32, name=f"a{e}{t}", tag=f"a{t}") for t in range(PACK)]
-            round_w1(e, 0, HEAD_ON_SCALAR[0] if e == 0 else PASS0_ON_SCALAR, 1)
-            if e > 0:
-                staged = w1_raw[e, 0][:, :CHUNKS, :C]
-                times_gate(e - 1, y_bank[:], staged)
-                for c in range(CHUNKS):
-                    scatter(e - 1, c, staged[:, c, :], False)
-            first_layer_pass(e, 0, banks, 1)
-            round_w1(e, 1, HEAD_ON_SCALAR[1] if e == 0 else 0, 2)
-            first_layer_pass(e, 1, banks, PACK if e == LAST else 2)
-            relu_squared(e, banks)
-            if e < LAST:
-                round_chunks(e, 0, CHUNKS)
-                quantise_chunks(e, 0, CHUNKS)
-                quantise_h(e)
-                y_bank = products(e, 0, CHUNKS, "y1")
-        round_chunks(LAST, 0, 1)
-        round_chunks(LAST, 1, CHUNKS)
-        quantise_chunks(LAST, 0, 1)
-        quantise_chunks(LAST, 1, CHUNKS)
-        quantise_h(LAST)
-        gated = sbuf("gated", [P, CHUNKS, C], F32)
-        times_gate(LAST, products(LAST, 0, 1, "y0")[:], gated[:, :1, :])
-        times_gate(LAST, products(LAST, 1, CHUNKS, "y2")[:], gated[:, 1:, :])
-        for c in range(CHUNKS):
-            scatter(LAST, c, gated[:, c, :], c == 1)
+            if e == LAST:
+                round_w1(on_vector, e, 0, slice(0, P), low)
+                round_w1(on_vector, e, 0, slice(0, P), high)
+                quantise(w1_op[e, 0], 0, H // 2)
+                quantise(w1_op[e, 0], H // 2, H)
+                quantise(h_op[e - 1][0], 0, C)
+            else:
+                cut = HEAD_ON_SCALAR if e == 0 else PASS0_ON_SCALAR
+                round_w1(on_scalar, e, 0, slice(0, cut), both)
+                round_w1(on_vector, e, 0, slice(cut, P), both)
+                if e > 0:
+                    staged = w1_raw[e, 0][:, :CHUNKS, :C]
+                    times_gate(e - 1, y_first[:], staged[:, :1, :])
+                    times_gate(e - 1, y_rest[:], staged[:, 1:, :])
+                    for c in range(CHUNKS):
+                        scatter(e - 1, c, staged[:, c, :], False)
+                quantise(w1_op[e, 0], 0, H)
+            first_layer(e, 0, banks, range(PACK))
+            cut = PASS1_ON_SCALAR if e in (0, LAST) else 0
+            if cut > 0:
+                round_w1(on_scalar, e, 1, slice(0, cut), both)
+            round_w1(on_vector, e, 1, slice(cut, P), low)
+            round_w1(on_vector, e, 1, slice(cut, P), high)
+            for a in range(0, H, H // 2):
+                quantise(w1_op[e, 1], a, a + H // 2)
+            first_layer(e, 1, banks, range(PACK))
+            relu = relu_squared(e, banks)
+            if e < LAST - 1:
+                round_w2(on_vector, e, 0, CHUNKS)
+                quantise(w2_op[e], 0, N)
+                quantise(h_op[e][0], 0, C)
+                y_first = second_layer(e, 0, 1, "y0")
+                y_rest = second_layer(e, 1, CHUNKS, "y1")
+
+        A, B = LAST - 1, LAST
+        gated = sbuf("gated", [P, 2 * CHUNKS, C], F32)
+
+        def chunk(e, c):
+            quantise(w2_op[e], c * P, (c + 1) * P)
+
+        def finish(e, c, tag, staged, by_vector):
+            times_gate(e, second_layer(e, c, c + 1, tag)[:], staged)
+            scatter(e, c, staged[:, 0, :], by_vector)
+
+        round_w2(on_vector, A, 0, 1)
+        round_w2(on_vector, A, 1, 2)
+        chunk(A, 0)
+        chunk(A, 1)
+        round_w2(on_vector, A, 2, 3)
+        finish(A, 0, "y0", gated[:, 0:1, :], False)
+        round_w2(on_vector, B, 0, 1)
+        quantise(h_op[B][0], 0, C)
+        finish(A, 1, "y1", gated[:, 1:2, :], False)
+        chunk(B, 0)
+        round_w2(on_vector, B, 1, 2)
+        chunk(A, 2)
+        finish(B, 0, "y2", gated[:, 2:3, :], False)
+        chunk(B, 1)
+        round_w2(on_vector, B, 2, 3)
+        late = w2_raw[B][:, 0:1, 2 * P :]
+        times_gate(A, second_layer(A, 2, 3, "y3")[:], late)
+        chunk(B, 2)
+        finish(B, 1, "a0", gated[:, 3:4, :], False)
+        scatter(A, 2, late[:, 0, :], True)
+        finish(B, 2, "a1", gated[:, 4:5, :], True)
         for c in range(CHUNKS):
             nc.sync.dma_start(out=out[c * P : (c + 1) * P, :], in_=out_sb[c][:])

@@ -28,9 +28,11 @@ LAST = E - 1
 SCALE_ROWS = 4
 RUN = 4
 
-HEAD_ON_SCALAR = 3 * P // 4
+EARLY = E - 2
+
+FIRST_PASS_ON_SCALAR = 3 * P // 4
 PASS0_ON_SCALAR = 3 * P // 8
-PASS1_ON_SCALAR = 3 * P // 8
+PASS1_ON_SCALAR = 3 * P // 4
 
 FLOPS = 2 * SLOTS * (K * H + H * N)
 
@@ -42,8 +44,8 @@ def tile_moe_two_mlp_relu2_kernel(tc, x_words, x_scales, w1, w2, gate, offs, dst
         keep = ctx.enter_context(tc.tile_pool(name="keep", bufs=1))
         psum = ctx.enter_context(tc.psum_pool(name="psum", bufs=1))
 
-        def sbuf(name, shape, dtype, tag=None):
-            return keep.tile(shape, dtype, name=name, tag=tag or name, align_bytes=64)
+        def sbuf(name, shape, dtype):
+            return keep.tile(shape, dtype, name=name, tag=name, align_bytes=64)
 
         offs_sb = keep.tile([P, SLOTS // PER_COL], U16, name="offs_sb")
         dst_sb = keep.tile([P, SLOTS // PER_COL], U16, name="dst_sb")
@@ -91,10 +93,10 @@ def tile_moe_two_mlp_relu2_kernel(tc, x_words, x_scales, w1, w2, gate, offs, dst
         for e in range(1, E):
             load_w1(e, 0)
             load_w1(e, 1)
-            if e < LAST - 1:
+            if e < EARLY:
                 load_w2(e)
-        load_w2(LAST - 1)
-        load_w2(LAST)
+        for e in range(EARLY, E):
+            load_w2(e)
 
         def spread_gate():
             spread = psum.tile([P, PACK, P], F32, name="gate_ps", tag="y0")
@@ -141,17 +143,19 @@ def tile_moe_two_mlp_relu2_kernel(tc, x_words, x_scales, w1, w2, gate, offs, dst
 
         w1_op = {(e, o): operand(f"w1_{e}{o}", H) for e in range(E) for o in range(PASSES)}
         w2_op = [operand(f"w2_{e}", N) for e in range(E)]
-        h_op = [(operand(f"h_{e}", C), 0) for e in range(E)]
+        h_op = [operand(f"h_{e}", C) for e in range(E)]
+
+        low, high, both = slice(0, PACK // 2), slice(PACK // 2, PACK), slice(0, PACK)
 
         def round_w1(copy, e, o, ms, ts):
             src = w1_raw[e, o][:].rearrange("p j (m t) -> p m j t", t=PACK)
-            dest = w1_op[e, o][0][:, :H, :].rearrange("p (t m) j -> p m j t", t=PACK)
+            dest = w1_op[e, o][0][:].rearrange("p (t m) j -> p m j t", t=PACK)
             copy(out=dest[:, ms, :, ts], in_=src[:, ms, :, ts])
 
-        def first_layer(e, o, banks, ts):
+        def first_layer(e, o, banks):
             slots = slice(e * C, (e + 1) * C)
             tokens = slot_words[o][:, slots].bitcast(FP8X4), slot_scales[SCALE_ROWS * o :, slots]
-            for t in ts:
+            for t in range(PACK):
                 product(banks[t][:], codes(w1_op[e, o], t * P), tokens, o == 0, o == PASSES - 1)
 
         def round_w2(copy, e, a, b):
@@ -160,50 +164,49 @@ def tile_moe_two_mlp_relu2_kernel(tc, x_words, x_scales, w1, w2, gate, offs, dst
 
         def relu_squared(e, banks):
             relu = sbuf(f"relu{e}", [P, PACK, C], F32)
-            op, first = h_op[e]
-            for t0 in range(0, PACK, 2):
-                for t in (t0, t0 + 1):
+            for pair in (low, high):
+                for t in range(pair.start, pair.stop):
                     nc.scalar.activation(out=relu[:, t, :], in_=banks[t][:], func=ACT.Relu)
                 nc.scalar.activation(
-                    out=op[0][:, first : first + C, t0 : t0 + 2].rearrange("p (g u) t -> p g t u", u=RUN),
-                    in_=relu[:, t0 : t0 + 2, :].rearrange("p t (g u) -> p g t u", u=RUN),
+                    out=h_op[e][0][:, :, pair].rearrange("p (g u) t -> p g t u", u=RUN),
+                    in_=relu[:, pair, :].rearrange("p t (g u) -> p g t u", u=RUN),
                     func=ACT.Square,
                 )
-            return relu
 
         def second_layer(e, a, b, tag):
             bank = psum.tile([P, b - a, C], F32, name=f"y{e}{a}", tag=tag)
             for c in range(a, b):
-                product(bank[:, c - a, :], codes(w2_op[e], c * P), codes(*h_op[e]), True, True)
+                product(bank[:, c - a, :], codes(w2_op[e], c * P), codes(h_op[e], 0), True, True)
             return bank
 
         def times_gate(e, sums, dest):
             weights = gate_sb[:, e * C : (e + 1) * C].unsqueeze(1).to_broadcast(list(sums.shape))
             nc.vector.tensor_tensor(dest, sums, weights, MULT)
 
-        def scatter(e, c, values, on_vector):
-            window = out_sb[c][:].indirect(dst_sb[:, e * C // PER_COL : (e + 1) * C // PER_COL])
-            if on_vector:
-                nc.vector.tensor_copy(window, values)
-            else:
-                nc.scalar.activation(out=window, in_=values, func=ACT.Copy)
+        def places(e, c):
+            return out_sb[c][:].indirect(dst_sb[:, e * C // PER_COL : (e + 1) * C // PER_COL])
+
+        def scatter_on_scalar(e, c, values):
+            nc.scalar.activation(out=places(e, c), in_=values, func=ACT.Copy)
+
+        def scatter_on_vector(e, c, values):
+            nc.vector.tensor_copy(places(e, c), values)
 
         on_scalar, on_vector = nc.scalar.copy, nc.vector.tensor_copy
-        low, high, both = slice(0, PACK // 2), slice(PACK // 2, PACK), slice(0, PACK)
         spread_gate()
         gather(0)
         gather(1)
         y_first = y_rest = None
         for e in range(E):
             banks = [psum.tile([P, C], F32, name=f"a{e}{t}", tag=f"a{t}") for t in range(PACK)]
-            if e == LAST:
+            if e > EARLY:
                 round_w1(on_vector, e, 0, slice(0, P), low)
                 round_w1(on_vector, e, 0, slice(0, P), high)
                 quantise(w1_op[e, 0], 0, H // 2)
                 quantise(w1_op[e, 0], H // 2, H)
-                quantise(h_op[e - 1][0], 0, C)
+                quantise(h_op[e - 1], 0, C)
             else:
-                cut = HEAD_ON_SCALAR if e == 0 else PASS0_ON_SCALAR
+                cut = FIRST_PASS_ON_SCALAR if e == 0 else PASS0_ON_SCALAR
                 round_w1(on_scalar, e, 0, slice(0, cut), both)
                 round_w1(on_vector, e, 0, slice(cut, P), both)
                 if e > 0:
@@ -211,55 +214,59 @@ def tile_moe_two_mlp_relu2_kernel(tc, x_words, x_scales, w1, w2, gate, offs, dst
                     times_gate(e - 1, y_first[:], staged[:, :1, :])
                     times_gate(e - 1, y_rest[:], staged[:, 1:, :])
                     for c in range(CHUNKS):
-                        scatter(e - 1, c, staged[:, c, :], False)
+                        scatter_on_scalar(e - 1, c, staged[:, c, :])
                 quantise(w1_op[e, 0], 0, H)
-            first_layer(e, 0, banks, range(PACK))
+            first_layer(e, 0, banks)
+
             cut = PASS1_ON_SCALAR if e in (0, LAST) else 0
             if cut > 0:
-                round_w1(on_scalar, e, 1, slice(0, cut), both)
-            round_w1(on_vector, e, 1, slice(cut, P), low)
+                round_w1(on_scalar, e, 1, slice(0, cut), high)
+            round_w1(on_vector, e, 1, slice(0, P), low)
             round_w1(on_vector, e, 1, slice(cut, P), high)
             for a in range(0, H, H // 2):
                 quantise(w1_op[e, 1], a, a + H // 2)
-            first_layer(e, 1, banks, range(PACK))
-            relu = relu_squared(e, banks)
-            if e < LAST - 1:
+            first_layer(e, 1, banks)
+            relu_squared(e, banks)
+            if e < EARLY:
                 round_w2(on_vector, e, 0, CHUNKS)
                 quantise(w2_op[e], 0, N)
-                quantise(h_op[e][0], 0, C)
+                quantise(h_op[e], 0, C)
                 y_first = second_layer(e, 0, 1, "y0")
                 y_rest = second_layer(e, 1, CHUNKS, "y1")
 
-        A, B = LAST - 1, LAST
-        gated = sbuf("gated", [P, 2 * CHUNKS, C], F32)
+        first, second = EARLY, LAST
+        gated = sbuf("gated", [P, 2 * CHUNKS - 1, C], F32)
 
-        def chunk(e, c):
+        def round_chunk(e, c):
+            round_w2(on_vector, e, c, c + 1)
+
+        def quantise_chunk(e, c):
             quantise(w2_op[e], c * P, (c + 1) * P)
 
-        def finish(e, c, tag, staged, by_vector):
+        def finish(e, c, tag, staged, scatter):
             times_gate(e, second_layer(e, c, c + 1, tag)[:], staged)
-            scatter(e, c, staged[:, 0, :], by_vector)
+            scatter(e, c, staged[:, 0, :])
 
-        round_w2(on_vector, A, 0, 1)
-        round_w2(on_vector, A, 1, 2)
-        chunk(A, 0)
-        chunk(A, 1)
-        round_w2(on_vector, A, 2, 3)
-        finish(A, 0, "y0", gated[:, 0:1, :], False)
-        round_w2(on_vector, B, 0, 1)
-        quantise(h_op[B][0], 0, C)
-        finish(A, 1, "y1", gated[:, 1:2, :], False)
-        chunk(B, 0)
-        round_w2(on_vector, B, 1, 2)
-        chunk(A, 2)
-        finish(B, 0, "y2", gated[:, 2:3, :], False)
-        chunk(B, 1)
-        round_w2(on_vector, B, 2, 3)
-        late = w2_raw[B][:, 0:1, 2 * P :]
-        times_gate(A, second_layer(A, 2, 3, "y3")[:], late)
-        chunk(B, 2)
-        finish(B, 1, "a0", gated[:, 3:4, :], False)
-        scatter(A, 2, late[:, 0, :], True)
-        finish(B, 2, "a1", gated[:, 4:5, :], True)
+        round_chunk(first, 0)
+        round_chunk(first, 1)
+        quantise_chunk(first, 0)
+        quantise_chunk(first, 1)
+        round_chunk(first, 2)
+        finish(first, 0, "y0", gated[:, 0:1, :], scatter_on_scalar)
+        round_chunk(second, 0)
+        quantise(h_op[second], 0, C)
+        finish(first, 1, "y1", gated[:, 1:2, :], scatter_on_scalar)
+        quantise_chunk(second, 0)
+        round_chunk(second, 1)
+        quantise_chunk(first, 2)
+        finish(second, 0, "y2", gated[:, 2:3, :], scatter_on_scalar)
+        quantise_chunk(second, 1)
+        round_chunk(second, 2)
+        late = w2_raw[second][:, 0:1, 2 * P :]
+        times_gate(first, second_layer(first, 2, 3, "y3")[:], late)
+        quantise_chunk(second, 2)
+        finish(second, 1, "a0", gated[:, 3:4, :], scatter_on_scalar)
+        scatter_on_vector(first, 2, late[:, 0, :])
+        finish(second, 2, "a1", gated[:, 4:5, :], scatter_on_vector)
         for c in range(CHUNKS):
             nc.sync.dma_start(out=out[c * P : (c + 1) * P, :], in_=out_sb[c][:])

@@ -32,7 +32,7 @@ EARLY = E - 2
 
 FIRST_PASS_ON_SCALAR = 3 * P // 4
 PASS0_ON_SCALAR = 3 * P // 8
-PASS1_ON_SCALAR = 3 * P // 4
+PASS1_ON_SCALAR = 3 * P // 8
 
 FLOPS = 2 * SLOTS * (K * H + H * N)
 
@@ -145,12 +145,24 @@ def tile_moe_two_mlp_relu2_kernel(tc, x_words, x_scales, w1, w2, gate, offs, dst
         w2_op = [operand(f"w2_{e}", N) for e in range(E)]
         h_op = [operand(f"h_{e}", C) for e in range(E)]
 
-        low, high, both = slice(0, PACK // 2), slice(PACK // 2, PACK), slice(0, PACK)
-
-        def round_w1(copy, e, o, ms, ts):
+        def w1_views(e, o):
             src = w1_raw[e, o][:].rearrange("p j (m t) -> p m j t", t=PACK)
-            dest = w1_op[e, o][0][:].rearrange("p (t m) j -> p m j t", t=PACK)
-            copy(out=dest[:, ms, :, ts], in_=src[:, ms, :, ts])
+            return src, w1_op[e, o][0][:].rearrange("p (t m) j -> p m j t", t=PACK)
+
+        def round_w1_shared(e, o, cut):
+            src, dest = w1_views(e, o)
+            nc.scalar.copy(out=dest[:, :cut], in_=src[:, :cut])
+            nc.vector.tensor_copy(out=dest[:, cut:], in_=src[:, cut:])
+
+        def round_w1_alone(e, o):
+            src, dest = w1_views(e, o)
+            for t in range(0, PACK, PACK // 2):
+                half = slice(t, t + PACK // 2)
+                nc.vector.tensor_copy(out=dest[:, :, :, half], in_=src[:, :, :, half])
+
+        def quantise_halves(e, o):
+            for a in range(0, H, H // 2):
+                quantise(w1_op[e, o], a, a + H // 2)
 
         def first_layer(e, o, banks):
             slots = slice(e * C, (e + 1) * C)
@@ -158,20 +170,19 @@ def tile_moe_two_mlp_relu2_kernel(tc, x_words, x_scales, w1, w2, gate, offs, dst
             for t in range(PACK):
                 product(banks[t][:], codes(w1_op[e, o], t * P), tokens, o == 0, o == PASSES - 1)
 
-        def round_w2(copy, e, a, b):
+        def round_w2(e, a, b):
             src = w2_raw[e][:, :, a * P : b * P].rearrange("p j (g u) -> p g j u", u=RUN)
-            copy(out=w2_op[e][0][:, a * P : b * P, :].rearrange("p (g u) j -> p g j u", u=RUN), in_=src)
+            nc.vector.tensor_copy(out=w2_op[e][0][:, a * P : b * P, :].rearrange("p (g u) j -> p g j u", u=RUN), in_=src)
 
         def relu_squared(e, banks):
             relu = sbuf(f"relu{e}", [P, PACK, C], F32)
-            for pair in (low, high):
-                for t in range(pair.start, pair.stop):
-                    nc.scalar.activation(out=relu[:, t, :], in_=banks[t][:], func=ACT.Relu)
-                nc.scalar.activation(
-                    out=h_op[e][0][:, :, pair].rearrange("p (g u) t -> p g t u", u=RUN),
-                    in_=relu[:, pair, :].rearrange("p t (g u) -> p g t u", u=RUN),
-                    func=ACT.Square,
-                )
+            for t in range(PACK):
+                nc.scalar.activation(out=relu[:, t, :], in_=banks[t][:], func=ACT.Relu)
+            nc.scalar.activation(
+                out=h_op[e][0][:].rearrange("p (g u) t -> p g t u", u=RUN),
+                in_=relu[:].rearrange("p t (g u) -> p g t u", u=RUN),
+                func=ACT.Square,
+            )
 
         def second_layer(e, a, b, tag):
             bank = psum.tile([P, b - a, C], F32, name=f"y{e}{a}", tag=tag)
@@ -192,7 +203,6 @@ def tile_moe_two_mlp_relu2_kernel(tc, x_words, x_scales, w1, w2, gate, offs, dst
         def scatter_on_vector(e, c, values):
             nc.vector.tensor_copy(places(e, c), values)
 
-        on_scalar, on_vector = nc.scalar.copy, nc.vector.tensor_copy
         spread_gate()
         gather(0)
         gather(1)
@@ -200,15 +210,12 @@ def tile_moe_two_mlp_relu2_kernel(tc, x_words, x_scales, w1, w2, gate, offs, dst
         for e in range(E):
             banks = [psum.tile([P, C], F32, name=f"a{e}{t}", tag=f"a{t}") for t in range(PACK)]
             if e > EARLY:
-                round_w1(on_vector, e, 0, slice(0, P), low)
-                round_w1(on_vector, e, 0, slice(0, P), high)
-                quantise(w1_op[e, 0], 0, H // 2)
-                quantise(w1_op[e, 0], H // 2, H)
+                round_w1_alone(e, 0)
+                quantise_halves(e, 0)
                 quantise(h_op[e - 1], 0, C)
             else:
                 cut = FIRST_PASS_ON_SCALAR if e == 0 else PASS0_ON_SCALAR
-                round_w1(on_scalar, e, 0, slice(0, cut), both)
-                round_w1(on_vector, e, 0, slice(cut, P), both)
+                round_w1_shared(e, 0, cut)
                 if e > 0:
                     staged = w1_raw[e, 0][:, :CHUNKS, :C]
                     times_gate(e - 1, y_first[:], staged[:, :1, :])
@@ -218,17 +225,15 @@ def tile_moe_two_mlp_relu2_kernel(tc, x_words, x_scales, w1, w2, gate, offs, dst
                 quantise(w1_op[e, 0], 0, H)
             first_layer(e, 0, banks)
 
-            cut = PASS1_ON_SCALAR if e in (0, LAST) else 0
-            if cut > 0:
-                round_w1(on_scalar, e, 1, slice(0, cut), high)
-            round_w1(on_vector, e, 1, slice(0, P), low)
-            round_w1(on_vector, e, 1, slice(cut, P), high)
-            for a in range(0, H, H // 2):
-                quantise(w1_op[e, 1], a, a + H // 2)
+            if e in (0, LAST):
+                round_w1_shared(e, 1, PASS1_ON_SCALAR)
+            else:
+                round_w1_alone(e, 1)
+            quantise_halves(e, 1)
             first_layer(e, 1, banks)
             relu_squared(e, banks)
             if e < EARLY:
-                round_w2(on_vector, e, 0, CHUNKS)
+                round_w2(e, 0, CHUNKS)
                 quantise(w2_op[e], 0, N)
                 quantise(h_op[e], 0, C)
                 y_first = second_layer(e, 0, 1, "y0")
@@ -238,7 +243,7 @@ def tile_moe_two_mlp_relu2_kernel(tc, x_words, x_scales, w1, w2, gate, offs, dst
         gated = sbuf("gated", [P, 2 * CHUNKS - 1, C], F32)
 
         def round_chunk(e, c):
-            round_w2(on_vector, e, c, c + 1)
+            round_w2(e, c, c + 1)
 
         def quantise_chunk(e, c):
             quantise(w2_op[e], c * P, (c + 1) * P)

@@ -32,7 +32,7 @@ EARLY = E - 2
 
 FIRST_PASS_ON_SCALAR = 3 * P // 4
 PASS0_ON_SCALAR = 3 * P // 8
-PASS1_ON_SCALAR = 3 * P // 8
+PASS1_ON_SCALAR = 5 * P // 16
 
 FLOPS = 2 * SLOTS * (K * H + H * N)
 
@@ -152,7 +152,12 @@ def tile_moe_two_mlp_relu2_kernel(tc, x_words, x_scales, w1, w2, gate, offs, dst
         def round_w1_shared(e, o, cut):
             src, dest = w1_views(e, o)
             nc.scalar.copy(out=dest[:, :cut], in_=src[:, :cut])
-            nc.vector.tensor_copy(out=dest[:, cut:], in_=src[:, cut:])
+            if o == 0:
+                nc.vector.tensor_copy(out=dest[:, cut:], in_=src[:, cut:])
+            else:
+                for t in range(0, PACK, PACK // 2):
+                    half = slice(t, t + PACK // 2)
+                    nc.vector.tensor_copy(out=dest[:, cut:, :, half], in_=src[:, cut:, :, half])
 
         def round_w1_alone(e, o):
             src, dest = w1_views(e, o)

from contextlib import ExitStack

import concourse.mybir as mybir
from concourse.masks import make_identity

K, T, E, C, H, N = 1024, 640, 4, 128, 512, 384

F32 = mybir.dt.float32
BF16 = mybir.dt.bfloat16
I32 = mybir.dt.int32
U32 = mybir.dt.uint32
U16 = mybir.dt.uint16
U8 = mybir.dt.uint8
FP8X4 = mybir.dt.float8_e4m3fn_x4
ACT = mybir.ActivationFunctionType
MULT = mybir.AluOpType.mult

P = 128
PACK = 4
PASSES = K // (P * PACK)
SLOTS = E * C
CHUNKS = N // P
PER_COL = 16
QUADRANT = 32
HALF = SLOTS // 2
LAST = E - 1

SCALE_ROWS = 4
RUN = 4

EARLY = E - 2

FIRST_PASS_ON_SCALAR = 3 * P // 4
PASS0_ON_SCALAR = 3 * P // 8
PASS1_ON_SCALAR = 5 * P // 16

FLOPS = 2 * SLOTS * (K * H + H * N)


def tile_moe_two_mlp_relu2_kernel(tc, x_words, x_scales, w1, w2, gate, offs, dst, out):
    nc = tc.nc

    with ExitStack() as ctx:
        keep = ctx.enter_context(tc.tile_pool(name="keep", bufs=1))
        psum = ctx.enter_context(tc.psum_pool(name="psum", bufs=1))

        def sbuf(name, shape, dtype):
            return keep.tile(shape, dtype, name=name, tag=name, align_bytes=64)

        offs_sb = keep.tile([P, SLOTS // PER_COL], U16, name="offs_sb")
        dst_sb = keep.tile([P, SLOTS // PER_COL], U16, name="dst_sb")
        tok_words = sbuf("tok_words", [P, PASSES * T], I32)
        tok_scales = sbuf("tok_scales", [P, T], U8)
        slot_words = [sbuf(f"slot_words{o}", [P, SLOTS], U32) for o in range(PASSES)]
        slot_scales = sbuf("slot_scales", [P, SLOTS], U8)
        gate_row = sbuf("gate_row", [P, PACK], F32)
        gate_sb = sbuf("gate_sb", [P, SLOTS], F32)
        ident = sbuf("ident", [P, P], F32)
        out_sb = [sbuf(f"out{c}", [P, T], F32) for c in range(CHUNKS)]

        nc.vector.memset(tok_scales[:].bitcast(I32), 0)
        make_identity(nc, ident[:])
        for c in range(CHUNKS):
            nc.gpsimd.memset(out_sb[c][:], 0.0)

        w1_raw = {}
        w2_raw = {}

        def load_w1(e, o):
            w1_raw[e, o] = sbuf(f"w1raw{e}{o}", [P, PACK, H], F32)
            rows = w1[e, o * P * PACK : (o + 1) * P * PACK, :]
            nc.sync.dma_start(out=w1_raw[e, o][:], in_=rows.rearrange("(p j) i -> p j i", j=PACK))

        def load_w2(e):
            w2_raw[e] = sbuf(f"w2raw{e}", [P, PACK, N], F32)
            nc.sync.dma_start(out=w2_raw[e][:], in_=w2[e].rearrange("(p j) n -> p j n", j=PACK))

        nc.sync.dma_start(
            out=tok_words[:].rearrange("p (o t) -> p o t", o=PASSES),
            in_=x_words.rearrange("o p t r -> p o (t r)").bitcast(I32),
        )
        nc.sync.dma_start(offs_sb[:], offs)
        load_w1(0, 0)
        for q in range(P // QUADRANT):
            nc.sync.dma_start(
                out=tok_scales[QUADRANT * q : QUADRANT * q + SCALE_ROWS * PASSES, :].bitcast(I32),
                in_=x_scales[:, SCALE_ROWS * q : SCALE_ROWS * (q + 1), :].bitcast(I32),
            )
        nc.sync.dma_start(out=gate_row[:], in_=gate[0, :].rearrange("(p j) -> p j", j=PACK))
        load_w1(0, 1)
        load_w2(0)
        nc.sync.dma_start(dst_sb[:], dst)
        for e in range(1, E):
            load_w1(e, 0)
            load_w1(e, 1)
            if e < EARLY:
                load_w2(e)
        for e in range(EARLY, E):
            load_w2(e)

        def spread_gate():
            spread = psum.tile([P, PACK, P], F32, name="gate_ps", tag="y0")
            for j in range(PACK):
                nc.tensor.transpose(spread[:, j, :], gate_row[:, j : j + 1].to_broadcast([P, P]), ident[:])
            nc.scalar.copy(out=gate_sb[:].rearrange("p (s j) -> p s j", j=PACK), in_=spread[:].rearrange("p j s -> p s j"))

        def gather(half):
            cols = slice(half * HALF, (half + 1) * HALF)
            entries = offs_sb[:, half * HALF // PER_COL : (half + 1) * HALF // PER_COL]
            for o in range(PASSES):
                window = tok_words[:, o * T : (o + 1) * T].bitcast(U32)
                nc.vector.tensor_copy(slot_words[o][:, cols], window.indirect(entries))
            nc.vector.tensor_copy(slot_scales[:, cols], tok_scales[:].indirect(entries))

        def operand(name, columns):
            return (
                sbuf(f"{name}_bf", [P, columns, PACK], BF16),
                sbuf(f"{name}_w", [P, columns], U32),
                sbuf(f"{name}_s", [P, columns], U8),
            )

        def quantise(op, first, last):
            rounded, words, scales = op
            nc.vector.quantize_mx(
                out=words[:, first:last].bitcast(FP8X4),
                scales=scales[:, first:last],
                in_=rounded[:, first:last, :].rearrange("p n j -> p (n j)"),
            )

        def codes(op, first):
            return op[1][:, first : first + P].bitcast(FP8X4), op[2][:, first : first + P]

        def product(dest, stationary, moving, start, stop):
            nc.tensor.matmul_mx(
                out=dest,
                lhsT=stationary[0],
                lhsT_scale=stationary[1],
                rhs=moving[0],
                rhs_scale=moving[1],
                start=start,
                stop=stop,
            )

        w1_op = {(e, o): operand(f"w1_{e}{o}", H) for e in range(E) for o in range(PASSES)}
        w2_op = [operand(f"w2_{e}", N) for e in range(E)]
        h_op = [operand(f"h_{e}", C) for e in range(E)]

        def w1_views(e, o):
            src = w1_raw[e, o][:].rearrange("p j (m t) -> p m j t", t=PACK)
            return src, w1_op[e, o][0][:].rearrange("p (t m) j -> p m j t", t=PACK)

        def round_w1_shared(e, o, cut):
            src, dest = w1_views(e, o)
            nc.scalar.copy(out=dest[:, :cut], in_=src[:, :cut])
            if o == 0:
                nc.vector.tensor_copy(out=dest[:, cut:], in_=src[:, cut:])
            else:
                for t in range(0, PACK, PACK // 2):
                    half = slice(t, t + PACK // 2)
                    nc.vector.tensor_copy(out=dest[:, cut:, :, half], in_=src[:, cut:, :, half])

        def round_w1_alone(e, o):
            src, dest = w1_views(e, o)
            for t in range(0, PACK, PACK // 2):
                half = slice(t, t + PACK // 2)
                nc.vector.tensor_copy(out=dest[:, :, :, half], in_=src[:, :, :, half])

        def quantise_halves(e, o):
            for a in range(0, H, H // 2):
                quantise(w1_op[e, o], a, a + H // 2)

        def first_layer(e, o, banks):
            slots = slice(e * C, (e + 1) * C)
            tokens = slot_words[o][:, slots].bitcast(FP8X4), slot_scales[SCALE_ROWS * o :, slots]
            for t in range(PACK):
                product(banks[t][:], codes(w1_op[e, o], t * P), tokens, o == 0, o == PASSES - 1)

        def round_w2(e, a, b):
            src = w2_raw[e][:, :, a * P : b * P].rearrange("p j (g u) -> p g j u", u=RUN)
            nc.vector.tensor_copy(out=w2_op[e][0][:, a * P : b * P, :].rearrange("p (g u) j -> p g j u", u=RUN), in_=src)

        def relu_squared(e, banks):
            relu = sbuf(f"relu{e}", [P, PACK, C], F32)
            for t in range(PACK):
                nc.scalar.activation(out=relu[:, t, :], in_=banks[t][:], func=ACT.Relu)
            nc.scalar.activation(
                out=h_op[e][0][:].rearrange("p (g u) t -> p g t u", u=RUN),
                in_=relu[:].rearrange("p t (g u) -> p g t u", u=RUN),
                func=ACT.Square,
            )

        def second_layer(e, a, b, tag):
            bank = psum.tile([P, b - a, C], F32, name=f"y{e}{a}", tag=tag)
            for c in range(a, b):
                product(bank[:, c - a, :], codes(w2_op[e], c * P), codes(h_op[e], 0), True, True)
            return bank

        def times_gate(e, sums, dest):
            weights = gate_sb[:, e * C : (e + 1) * C].unsqueeze(1).to_broadcast(list(sums.shape))
            nc.vector.tensor_tensor(dest, sums, weights, MULT)

        def places(e, c):
            return out_sb[c][:].indirect(dst_sb[:, e * C // PER_COL : (e + 1) * C // PER_COL])

        def scatter_on_scalar(e, c, values):
            nc.scalar.activation(out=places(e, c), in_=values, func=ACT.Copy)

        def scatter_on_vector(e, c, values):
            nc.vector.tensor_copy(places(e, c), values)

        spread_gate()
        gather(0)
        gather(1)
        y_first = y_rest = None
        for e in range(E):
            banks = [psum.tile([P, C], F32, name=f"a{e}{t}", tag=f"a{t}") for t in range(PACK)]
            if e > EARLY:
                round_w1_alone(e, 0)
                quantise_halves(e, 0)
                quantise(h_op[e - 1], 0, C)
            else:
                cut = FIRST_PASS_ON_SCALAR if e == 0 else PASS0_ON_SCALAR
                round_w1_shared(e, 0, cut)
                if e > 0:
                    staged = w1_raw[e, 0][:, :CHUNKS, :C]
                    times_gate(e - 1, y_first[:], staged[:, :1, :])
                    times_gate(e - 1, y_rest[:], staged[:, 1:, :])
                    for c in range(CHUNKS):
                        scatter_on_scalar(e - 1, c, staged[:, c, :])
                quantise(w1_op[e, 0], 0, H)
            first_layer(e, 0, banks)

            if e in (0, LAST):
                round_w1_shared(e, 1, PASS1_ON_SCALAR)
            else:
                round_w1_alone(e, 1)
            quantise_halves(e, 1)
            first_layer(e, 1, banks)
            relu_squared(e, banks)
            if e < EARLY:
                round_w2(e, 0, CHUNKS)
                quantise(w2_op[e], 0, N)
                quantise(h_op[e], 0, C)
                y_first = second_layer(e, 0, 1, "y0")
                y_rest = second_layer(e, 1, CHUNKS, "y1")

        first, second = EARLY, LAST
        gated = sbuf("gated", [P, 2 * CHUNKS - 1, C], F32)

        def round_chunk(e, c):
            round_w2(e, c, c + 1)

        def quantise_chunk(e, c):
            quantise(w2_op[e], c * P, (c + 1) * P)

        def finish(e, c, tag, staged, scatter):
            times_gate(e, second_layer(e, c, c + 1, tag)[:], staged)
            scatter(e, c, staged[:, 0, :])

        round_chunk(first, 0)
        round_chunk(first, 1)
        quantise_chunk(first, 0)
        quantise_chunk(first, 1)
        round_chunk(first, 2)
        finish(first, 0, "y0", gated[:, 0:1, :], scatter_on_scalar)
        round_chunk(second, 0)
        quantise(h_op[second], 0, C)
        finish(first, 1, "y1", gated[:, 1:2, :], scatter_on_scalar)
        quantise_chunk(second, 0)
        round_chunk(second, 1)
        quantise_chunk(first, 2)
        finish(second, 0, "y2", gated[:, 2:3, :], scatter_on_scalar)
        quantise_chunk(second, 1)
        round_chunk(second, 2)
        late = w2_raw[second][:, 0:1, 2 * P :]
        times_gate(first, second_layer(first, 2, 3, "y3")[:], late)
        quantise_chunk(second, 2)
        finish(second, 1, "a0", gated[:, 3:4, :], scatter_on_scalar)
        scatter_on_vector(first, 2, late[:, 0, :])
        finish(second, 2, "a1", gated[:, 4:5, :], scatter_on_vector)
        for c in range(CHUNKS):
            nc.sync.dma_start(out=out[c * P : (c + 1) * P, :], in_=out_sb[c][:])
